import numpy as np
import ml_dtypes


def mxq(x, axis, fmt="e4m3"):
    dtype, down = {"e4m3": (ml_dtypes.float8_e4m3fn, 7), "e5m2": (ml_dtypes.float8_e5m2, 14)}[fmt]
    v = np.moveaxis(np.asarray(x, np.float32).astype(ml_dtypes.bfloat16).astype(np.float64), axis, -1)
    blocks = v.reshape(v.shape[:-1] + (-1, 32))
    amax = np.abs(blocks).max(-1, keepdims=True)
    byte = np.maximum(np.where(amax > 0, np.frexp(amax)[1] - 1 + 127, 0) - down, 1)
    scale = np.exp2(byte - 127.0)
    codes = (blocks / scale).astype(np.float32).astype(dtype).astype(np.float64)
    return np.moveaxis((codes * scale).reshape(v.shape), -1, axis)


WIDE = False


def mx_kscale(k):
    if not WIDE:
        return np.ones(k)
    levels = np.array([10, -10, 5, -5, 0])
    if k % 512:
        return np.exp2(np.random.permutation(np.resize(levels, k // 32))).repeat(32)
    a = np.empty((k // 512, 16))
    for p in range(k // 512):
        a[p, :8] = np.random.permutation(np.resize(levels, 8))
        for g in range(8):
            far = levels[np.abs(levels - a[p, g]) >= 10]
            a[p, g + 8] = far[np.random.randint(len(far))]
    return np.exp2(a.ravel()).repeat(32)


def f64(x):
    return np.asarray(x).astype(np.float64)


def striped(idx):
    return np.tile(idx.reshape(-1, 16).T, (8, 1)).astype(np.uint16)


def unstriped(offs):
    return offs[:16].T.reshape(-1).astype(np.int64)


def relu(v):
    return np.maximum(v, 0.0)


K, T, E, C, H, N = 1024, 1024, 4, 128, 512, 512


def by_expert(wq, xq):
    return np.concatenate([wq[e].T @ xq[:, e * C:(e + 1) * C] for e in range(E)], axis=1)


def setup_inputs():
    n = np.random.standard_normal
    s = mx_kscale(K)[:, None]
    u = mx_kscale(H)
    return {
        "xT": (n((K, T)) * s).astype(np.float32),
        "xr": n((N, T)).astype(np.float32),
        "w1": (n((E, K, H)) / np.sqrt(K) / s[None] * u[None, None, :]).astype(np.float32),
        "w2": (n((E, H, N)) / np.sqrt(H) / u[None, :, None]).astype(np.float32),
        "gate": np.tile(np.random.uniform(0.2, 1.0, E * C), (N, 1)).astype(np.float32),
        "offs": striped(np.random.permutation(T)[:E * C]),
    }


def reference(xT, xr, w1, w2, gate, offs):
    idx = unstriped(offs)
    xq = mxq(f64(xT)[:, idx], 0, "e4m3")
    h = relu(by_expert(mxq(f64(w1), 1, "e4m3"), xq))
    y = by_expert(mxq(f64(w2), 1, "e4m3"), mxq(h, 0, "e4m3"))
    out = f64(xr).copy()
    out[:, idx] += f64(gate) * y
    return out

@@ -1,0 +1,274 @@
+from contextlib import ExitStack
+
+import concourse.mybir as mybir
+
+K, T, E, C, H, N = 1024, 1024, 4, 128, 512, 512
+S = E * C
+FLOPS = 2 * S * (K * H + H * N)
+
+F32 = mybir.dt.float32
+BF16 = mybir.dt.bfloat16
+U32 = mybir.dt.uint32
+U16 = mybir.dt.uint16
+U8 = mybir.dt.uint8
+FP8X4 = mybir.dt.float8_e4m3fn_x4
+ADD = mybir.AluOpType.add
+MULT = mybir.AluOpType.mult
+RELU = mybir.ActivationFunctionType.Relu
+
+P = 128
+J = 4
+K_PASS = P * J
+PASSES = K // K_PASS
+COLS = 512
+HALF = COLS // 2
+NT = N // P
+
+LOADS = (
+    ("xT", 0, 0),
+    ("xT", 0, 1),
+    ("offs",),
+    ("xT", 1, 0),
+    ("xT", 1, 1),
+    ("w2", 0, 0, COLS),
+    ("w1", 0, 0),
+    ("w1", 0, 1),
+    ("w1", 1, 0),
+    ("w1", 1, 1),
+    ("w2", 1, 0, COLS),
+    ("gate", 0),
+    ("w2", 2, 0, COLS),
+    ("w1", 2, 0),
+    ("w1", 2, 1),
+    ("w1", 3, 0),
+    ("gate", 1),
+    ("w1", 3, 1),
+    ("gate", 2),
+    ("w2", 3, 0, HALF),
+    ("xr", 0),
+    ("w2", 3, HALF, HALF),
+    ("gate", 3),
+    ("xr", 1),
+    ("xr", 2),
+    ("xr", 3),
+)
+
+VECTOR_EIGHTHS = {
+    ("xT", 0, 0): 7,
+    ("xT", 0, 1): 7,
+    ("xT", 1, 0): 2,
+    ("xT", 1, 1): 1,
+    ("w1", 0, 0): 0,
+    ("w1", 0, 1): 2,
+    ("w1", 1, 0): 3,
+    ("w1", 1, 1): 2,
+    ("w1", 2, 0): 4,
+    ("w1", 2, 1): 2,
+    ("w1", 3, 0): 1,
+    ("w1", 3, 1): 0,
+    ("w2", 0, 0, COLS): 6,
+    ("w2", 1, 0, COLS): 1,
+    ("w2", 2, 0, COLS): 4,
+    ("w2", 3, 0, HALF): 0,
+    ("w2", 3, HALF, HALF): 0,
+}
+
+
+def tile_moe_res_mlp_relu_kernel(tc, xT, xr, w1, w2, gate, offs, out):
+    nc = tc.nc
+    with ExitStack() as ctx:
+        keep = ctx.enter_context(tc.tile_pool(name="keep", bufs=1))
+        big = ctx.enter_context(tc.tile_pool(name="big", bufs=2))
+        raws = ctx.enter_context(tc.tile_pool(name="raws", bufs=9))
+        halves = ctx.enter_context(tc.tile_pool(name="halves", bufs=2))
+        psum = ctx.enter_context(tc.psum_pool(name="psum", bufs=1))
+
+        offsets = keep.tile([P, S // 16], U16, name="offsets")
+        gates = [keep.tile([P, C], F32, name=f"gates{e}") for e in range(E)]
+        x_codes = [keep.tile([P, T], U32, name=f"x_codes{s}", align_bytes=64) for s in range(PASSES)]
+        slot_codes = [keep.tile([P, S], U32, name=f"slot_codes{s}", align_bytes=64) for s in range(PASSES)]
+        x_scales = keep.tile([P, T], U8, name="x_scales", align_bytes=64)
+        slot_scales = keep.tile([P, S], U8, name="slot_scales", align_bytes=64)
+        w1_codes = [
+            [keep.tile([P, H], U32, name=f"w1_codes{e}_{s}", align_bytes=64) for s in range(PASSES)] for e in range(E)
+        ]
+        w1_scales = [
+            [keep.tile([P, H], U8, name=f"w1_scales{e}_{s}", align_bytes=64) for s in range(PASSES)] for e in range(E)
+        ]
+        w2_codes = [keep.tile([P, N], U32, name=f"w2_codes{e}", align_bytes=64) for e in range(E)]
+        w2_scales = [keep.tile([P, N], U8, name=f"w2_scales{e}", align_bytes=64) for e in range(E)]
+        windows = [keep.tile([P, T], F32, name=f"window{n}") for n in range(NT)]
+        x_raw = []
+        for s in range(PASSES):
+            x_tile = big.tile([P, J, T], F32, name="big")
+            x_raw.append(x_tile)
+        residual = big.tile([P, NT, T], F32, name="big")
+
+        table = keep.tile([P, 2], F32, name="table")
+        nc.vector.memset(table[:], 0.0)
+        nc.scalar.activation(out=table[:, 1:2], in_=table[:, 0:1], func=RELU)
+        nc.gpsimd.memset(x_scales[:], 0)
+        for n in range(NT):
+            nc.gpsimd.memset(windows[n][:], 0.0)
+
+        w_raw = {}
+
+        def rows_by_four(matrix):
+            return matrix.rearrange("(p j) c -> p j c", j=J)
+
+        def load(piece):
+            kind = piece[0]
+            if kind == "offs":
+                nc.sync.dma_start(offsets[:], offs)
+            elif kind == "gate":
+                e = piece[1]
+                nc.sync.dma_start(out=gates[e][:], in_=gate[0:P, e * C : (e + 1) * C])
+            elif kind == "xr":
+                n = piece[1]
+                nc.sync.dma_start(out=residual[:, n, :], in_=xr[n * P : (n + 1) * P, :])
+            elif kind == "xT":
+                s, half = piece[1:]
+                rows = slice(2 * half, 2 * half + 2)
+                source = rows_by_four(xT[s * K_PASS : (s + 1) * K_PASS, :])
+                nc.sync.dma_start(out=x_raw[s][:, rows, :], in_=source[:, rows, :])
+            elif kind == "w1":
+                e, s = piece[1:]
+                raw = raws.tile([P, J, COLS], F32, name="raw")
+                nc.sync.dma_start(out=raw[:], in_=rows_by_four(w1[e][s * K_PASS : (s + 1) * K_PASS, :]))
+                w_raw[piece] = raw
+            else:
+                e, first, columns = piece[1:]
+                if columns == COLS:
+                    raw = raws.tile([P, J, COLS], F32, name="raw")
+                else:
+                    raw = halves.tile([P, J, HALF], F32, name="raw_half")
+                nc.sync.dma_start(out=raw[:], in_=rows_by_four(w2[e][:, first : first + columns]))
+                w_raw[piece] = raw
+
+        def interleave(piece):
+            kind = piece[0]
+            if kind == "xT":
+                s, half = piece[1:]
+                source = x_raw[s][:, :, half * COLS : (half + 1) * COLS]
+                columns = COLS
+            else:
+                source = w_raw[piece][:]
+                columns = piece[3] if kind == "w2" else COLS
+            if kind == "w1" and piece[1] >= 2:
+                tag = f"{piece[1] - 2}_{piece[2]}"
+            elif kind == "xT":
+                tag = f"{piece[1]}_{piece[2]}"
+            else:
+                tag = f"{kind}_{piece[1]}_{piece[2]}"
+            grouped = keep.tile([P, columns * J], BF16, name="grouped_" + tag, align_bytes=64)
+            if kind == "w1":
+                target = grouped[:].rearrange("p (t m j) -> p m j t", t=4, j=J)
+                source = source.rearrange("p j (m t) -> p m j t", t=4)
+            else:
+                target = grouped[:].rearrange("p (c i j) -> p c j i", i=4, j=J)
+                source = source.rearrange("p j (c i) -> p c j i", i=4)
+            runs = columns // 4
+            cut = runs - runs * VECTOR_EIGHTHS[piece] // 8
+            if cut > 0:
+                nc.scalar.copy(out=target[:, :cut], in_=source[:, :cut])
+            if cut < runs:
+                nc.vector.tensor_copy(out=target[:, cut:], in_=source[:, cut:])
+            return grouped
+
+        def quantise(grouped, codes, scales):
+            nc.vector.quantize_mx(out=codes.bitcast(FP8X4), scales=scales, in_=grouped[:])
+
+        def first_layer(e):
+            slots = slice(e * C, (e + 1) * C)
+            acc = psum.tile([P, J, C], F32, name=f"acc1_{e % 2}")
+            for t in range(J):
+                channels = slice(t * P, (t + 1) * P)
+                for s in range(PASSES):
+                    nc.tensor.matmul_mx(
+                        out=acc[:, t, :],
+                        lhsT=w1_codes[e][s][:, channels].bitcast(FP8X4),
+                        lhsT_scale=w1_scales[e][s][:, channels],
+                        rhs=slot_codes[s][:, slots].bitcast(FP8X4),
+                        rhs_scale=slot_scales[4 * s : P, slots],
+                        start=(s == 0),
+                        stop=(s == PASSES - 1),
+                    )
+            hidden = keep.tile([P, C * J], BF16, name=f"hidden_{e}", align_bytes=64)
+            nc.scalar.activation(
+                out=hidden[:].rearrange("p (c t) -> p c t", t=J),
+                in_=acc[:].rearrange("p t c -> p c t"),
+                func=RELU,
+            )
+            codes = keep.tile([P, C], U32, name=f"h_codes_{e}", align_bytes=64)
+            scales = keep.tile([P, C], U8, name=f"h_scales_{e}", align_bytes=64)
+            quantise(hidden, codes[:], scales[:])
+            return codes, scales
+
+        def second_layer(e, h, tiles):
+            codes, scales = h
+            acc = psum.tile([P, len(tiles), C], F32, name=f"acc2_{e}_{tiles[0]}")
+            for i, n in enumerate(tiles):
+                rows = slice(n * P, (n + 1) * P)
+                nc.tensor.matmul_mx(
+                    out=acc[:, i, :],
+                    lhsT=w2_codes[e][:, rows].bitcast(FP8X4),
+                    lhsT_scale=w2_scales[e][:, rows],
+                    rhs=codes[:].bitcast(FP8X4),
+                    rhs_scale=scales[:],
+                    start=True,
+                    stop=True,
+                )
+            result = keep.tile([P, len(tiles), C], F32, name=f"y_{e}_{tiles[0]}")
+            nc.scalar.copy(out=result[:], in_=acc[:])
+            for i, n in enumerate(tiles):
+                y[(e, n)] = result[:, i, :]
+
+        def scatter(e, n):
+            nc.vector.tensor_tensor(
+                windows[n][:].indirect(offsets[:, e * (C // 16) : (e + 1) * (C // 16)]),
+                y[(e, n)],
+                gates[e][:],
+                MULT,
+            )
+
+        for piece in LOADS:
+            load(piece)
+
+        h = {}
+        y = {}
+        waiting = []
+        for piece in LOADS:
+            kind = piece[0]
+            if kind == "xT":
+                s, half = piece[1:]
+                tokens = slice(half * COLS, (half + 1) * COLS)
+                quantise(interleave(piece), x_codes[s][:, tokens], x_scales[4 * s : P, tokens])
+                if half == 1:
+                    nc.vector.tensor_copy(slot_codes[s][:], x_codes[s][:].indirect(offsets[:]))
+                    if s == PASSES - 1:
+                        nc.vector.tensor_copy(slot_scales[:], x_scales[:].indirect(offsets[:]))
+            elif kind == "w1":
+                e, s = piece[1:]
+                quantise(interleave(piece), w1_codes[e][s][:], w1_scales[e][s][:])
+                if s == PASSES - 1:
+                    h[e] = first_layer(e)
+            elif kind == "w2":
+                e, first, columns = piece[1:]
+                rows = slice(first, first + columns)
+                quantise(interleave(piece), w2_codes[e][:, rows], w2_scales[e][:, rows])
+                waiting.append((e, range(first // P, (first + columns) // P)))
+            for e, tiles in list(waiting):
+                if e in h:
+                    second_layer(e, h[e], tiles)
+                    waiting.remove((e, tiles))
+
+        for e in range(E - 1):
+            for n in range(NT):
+                scatter(e, n)
+        for n in range(NT):
+            rows = slice(n * P, (n + 1) * P)
+            scatter(E - 1, n)
+            for half in range(2):
+                tokens = slice(half * T // 2, (half + 1) * T // 2)
+                nc.vector.tensor_tensor(residual[:, n, tokens], windows[n][:, tokens], residual[:, n, tokens], ADD)
+                nc.sync.dma_start(out=out[rows, tokens], in_=residual[:, n, tokens])

@@ -20,58 +20,12 @@ P = 128
 J = 4
 K_PASS = P * J
 PASSES = K // K_PASS
-COLS = 512
-HALF = COLS // 2
 NT = N // P
 
-LOADS = (
-    ("xT", 0, 0),
-    ("xT", 0, 1),
-    ("offs",),
-    ("xT", 1, 0),
-    ("xT", 1, 1),
-    ("w2", 0, 0, COLS),
-    ("w1", 0, 0),
-    ("w1", 0, 1),
-    ("w1", 1, 0),
-    ("w1", 1, 1),
-    ("w2", 1, 0, COLS),
-    ("gate", 0),
-    ("w2", 2, 0, COLS),
-    ("w1", 2, 0),
-    ("w1", 2, 1),
-    ("w1", 3, 0),
-    ("gate", 1),
-    ("w1", 3, 1),
-    ("gate", 2),
-    ("w2", 3, 0, HALF),
-    ("xr", 0),
-    ("w2", 3, HALF, HALF),
-    ("gate", 3),
-    ("xr", 1),
-    ("xr", 2),
-    ("xr", 3),
-)
-
-VECTOR_EIGHTHS = {
-    ("xT", 0, 0): 7,
-    ("xT", 0, 1): 7,
-    ("xT", 1, 0): 2,
-    ("xT", 1, 1): 1,
-    ("w1", 0, 0): 0,
-    ("w1", 0, 1): 2,
-    ("w1", 1, 0): 3,
-    ("w1", 1, 1): 2,
-    ("w1", 2, 0): 4,
-    ("w1", 2, 1): 2,
-    ("w1", 3, 0): 1,
-    ("w1", 3, 1): 0,
-    ("w2", 0, 0, COLS): 6,
-    ("w2", 1, 0, COLS): 1,
-    ("w2", 2, 0, COLS): 4,
-    ("w2", 3, 0, HALF): 0,
-    ("w2", 3, HALF, HALF): 0,
-}
+X_SCALAR = 44
+W1_VECTOR = (32, 64)
+W2_VECTOR = 0
+A_CUT = 64
 
 
 def tile_moe_res_mlp_relu_kernel(tc, xT, xr, w1, w2, gate, offs, out):
@@ -79,30 +33,20 @@ def tile_moe_res_mlp_relu_kernel(tc, xT, xr, w1, w2, gate, offs, out):
     with ExitStack() as ctx:
         keep = ctx.enter_context(tc.tile_pool(name="keep", bufs=1))
         big = ctx.enter_context(tc.tile_pool(name="big", bufs=2))
-        raws = ctx.enter_context(tc.tile_pool(name="raws", bufs=9))
-        halves = ctx.enter_context(tc.tile_pool(name="halves", bufs=2))
+        ring = ctx.enter_context(tc.tile_pool(name="ring", bufs=2))
+        first = ctx.enter_context(tc.tile_pool(name="first", bufs=1))
         psum = ctx.enter_context(tc.psum_pool(name="psum", bufs=1))
 
         offsets = keep.tile([P, S // 16], U16, name="offsets")
-        gates = [keep.tile([P, C], F32, name=f"gates{e}") for e in range(E)]
+        gates = keep.tile([P, S], F32, name="gates")
         x_codes = [keep.tile([P, T], U32, name=f"x_codes{s}", align_bytes=64) for s in range(PASSES)]
-        slot_codes = [keep.tile([P, S], U32, name=f"slot_codes{s}", align_bytes=64) for s in range(PASSES)]
         x_scales = keep.tile([P, T], U8, name="x_scales", align_bytes=64)
-        slot_scales = keep.tile([P, S], U8, name="slot_scales", align_bytes=64)
-        w1_codes = [
-            [keep.tile([P, H], U32, name=f"w1_codes{e}_{s}", align_bytes=64) for s in range(PASSES)] for e in range(E)
-        ]
-        w1_scales = [
-            [keep.tile([P, H], U8, name=f"w1_scales{e}_{s}", align_bytes=64) for s in range(PASSES)] for e in range(E)
-        ]
-        w2_codes = [keep.tile([P, N], U32, name=f"w2_codes{e}", align_bytes=64) for e in range(E)]
-        w2_scales = [keep.tile([P, N], U8, name=f"w2_scales{e}", align_bytes=64) for e in range(E)]
         windows = [keep.tile([P, T], F32, name=f"window{n}") for n in range(NT)]
-        x_raw = []
-        for s in range(PASSES):
-            x_tile = big.tile([P, J, T], F32, name="big")
-            x_raw.append(x_tile)
+        x_raw = [big.tile([P, J, T], F32, name="big") for s in range(PASSES)]
         residual = big.tile([P, NT, T], F32, name="big")
+        w1_raw = [first.tile([P, PASSES, J, H], F32, name="w1_raw0", align_bytes=64, offset=0)]
+        w1_raw.extend(keep.tile([P, PASSES, J, H], F32, name=f"w1_raw{e}") for e in range(1, E))
+        w2_raw = [keep.tile([P, J, N], F32, name=f"w2_raw{e}", align_bytes=64) for e in range(E)]
 
         table = keep.tile([P, 2], F32, name="table")
         nc.vector.memset(table[:], 0.0)
@@ -111,164 +55,191 @@ def tile_moe_res_mlp_relu_kernel(tc, xT, xr, w1, w2, gate, offs, out):
         for n in range(NT):
             nc.gpsimd.memset(windows[n][:], 0.0)
 
-        w_raw = {}
-
         def rows_by_four(matrix):
             return matrix.rearrange("(p j) c -> p j c", j=J)
 
-        def load(piece):
-            kind = piece[0]
-            if kind == "offs":
-                nc.sync.dma_start(offsets[:], offs)
-            elif kind == "gate":
-                e = piece[1]
-                nc.sync.dma_start(out=gates[e][:], in_=gate[0:P, e * C : (e + 1) * C])
-            elif kind == "xr":
-                n = piece[1]
-                nc.sync.dma_start(out=residual[:, n, :], in_=xr[n * P : (n + 1) * P, :])
-            elif kind == "xT":
-                s, half = piece[1:]
+        for s in range(PASSES):
+            source = rows_by_four(xT[s * K_PASS : (s + 1) * K_PASS, :])
+            for half in range(2):
                 rows = slice(2 * half, 2 * half + 2)
-                source = rows_by_four(xT[s * K_PASS : (s + 1) * K_PASS, :])
                 nc.sync.dma_start(out=x_raw[s][:, rows, :], in_=source[:, rows, :])
-            elif kind == "w1":
-                e, s = piece[1:]
-                raw = raws.tile([P, J, COLS], F32, name="raw")
-                nc.sync.dma_start(out=raw[:], in_=rows_by_four(w1[e][s * K_PASS : (s + 1) * K_PASS, :]))
-                w_raw[piece] = raw
-            else:
-                e, first, columns = piece[1:]
-                if columns == COLS:
-                    raw = raws.tile([P, J, COLS], F32, name="raw")
-                else:
-                    raw = halves.tile([P, J, HALF], F32, name="raw_half")
-                nc.sync.dma_start(out=raw[:], in_=rows_by_four(w2[e][:, first : first + columns]))
-                w_raw[piece] = raw
-
-        def interleave(piece):
-            kind = piece[0]
-            if kind == "xT":
-                s, half = piece[1:]
-                source = x_raw[s][:, :, half * COLS : (half + 1) * COLS]
-                columns = COLS
-            else:
-                source = w_raw[piece][:]
-                columns = piece[3] if kind == "w2" else COLS
-            if kind == "w1" and piece[1] >= 2:
-                tag = f"{piece[1] - 2}_{piece[2]}"
-            elif kind == "xT":
-                tag = f"{piece[1]}_{piece[2]}"
-            else:
-                tag = f"{kind}_{piece[1]}_{piece[2]}"
-            grouped = keep.tile([P, columns * J], BF16, name="grouped_" + tag, align_bytes=64)
-            if kind == "w1":
-                target = grouped[:].rearrange("p (t m j) -> p m j t", t=4, j=J)
-                source = source.rearrange("p j (m t) -> p m j t", t=4)
-            else:
-                target = grouped[:].rearrange("p (c i j) -> p c j i", i=4, j=J)
-                source = source.rearrange("p j (c i) -> p c j i", i=4)
-            runs = columns // 4
-            cut = runs - runs * VECTOR_EIGHTHS[piece] // 8
-            if cut > 0:
-                nc.scalar.copy(out=target[:, :cut], in_=source[:, :cut])
-            if cut < runs:
-                nc.vector.tensor_copy(out=target[:, cut:], in_=source[:, cut:])
-            return grouped
+            if s == 0:
+                nc.sync.dma_start(offsets[:], offs)
+        for e in range(E):
+            for s in range(PASSES):
+                nc.sync.dma_start(out=w1_raw[e][:, s], in_=rows_by_four(w1[e][s * K_PASS : (s + 1) * K_PASS, :]))
+            nc.sync.dma_start(out=w2_raw[e][:], in_=rows_by_four(w2[e]))
+            if e == 0:
+                nc.sync.dma_start(out=gates[:], in_=gate[0:P, :])
+        for n in range(NT):
+            nc.sync.dma_start(out=residual[:, n, :], in_=xr[n * P : (n + 1) * P, :])
 
         def quantise(grouped, codes, scales):
-            nc.vector.quantize_mx(out=codes.bitcast(FP8X4), scales=scales, in_=grouped[:])
+            nc.vector.quantize_mx(out=codes.bitcast(FP8X4), scales=scales, in_=grouped)
 
-        def first_layer(e):
-            slots = slice(e * C, (e + 1) * C)
+        def slot_offsets(first_slot, end_slot):
+            return offsets[:, first_slot // 16 : end_slot // 16]
+
+        half_t = T // 2
+        codes_pass0 = keep.tile([P, S], U32, name="codes_pass0", align_bytes=64)
+        codes_first = keep.tile([P, C], U32, name="codes_first", align_bytes=64)
+        scales_first = keep.tile([P, C], U8, name="scales_first", align_bytes=64)
+        for s in range(PASSES):
+            for half in range(2):
+                tokens = slice(half * half_t, (half + 1) * half_t)
+                grouped = ring.tile([P, half_t * J], BF16, name="x_grouped", align_bytes=64)
+                target = grouped[:].rearrange("p (c i j) -> p c j i", i=4, j=J)
+                source = x_raw[s][:, :, tokens].rearrange("p j (c i) -> p c j i", i=4)
+                nc.scalar.copy(out=target[:, :X_SCALAR], in_=source[:, :X_SCALAR])
+                nc.vector.tensor_copy(out=target[:, X_SCALAR:], in_=source[:, X_SCALAR:])
+                quantise(grouped[:], x_codes[s][:, tokens], x_scales[4 * s : P, tokens])
+            if s == 0:
+                nc.vector.tensor_copy(codes_pass0[:], x_codes[0][:].indirect(offsets[:]))
+        nc.vector.tensor_copy(codes_first[:], x_codes[1][:].indirect(slot_offsets(0, C)))
+        nc.vector.tensor_copy(scales_first[:], x_scales[:].indirect(slot_offsets(0, C)))
+        codes_rest = first.tile([P, S - C], U32, name="codes_rest", align_bytes=64, offset=0)
+        scales_rest = first.tile([P, S - C], U8, name="scales_rest", align_bytes=64, offset=(S - C) * 4)
+
+        def slot_operand(e, s):
+            if e == 0:
+                codes = codes_first[:]
+                scales = scales_first[4 * s : P, :]
+            else:
+                codes = codes_rest[:, (e - 1) * C : e * C]
+                scales = scales_rest[4 * s : P, (e - 1) * C : e * C]
+            if s == 0:
+                codes = codes_pass0[:, e * C : (e + 1) * C]
+            return codes, scales
+
+        def round_w1(copy, e, s, grouped, first_run, end_run):
+            target = grouped[:, s].rearrange("p (t m j) -> p m j t", t=4, j=J)
+            source = w1_raw[e][:, s].rearrange("p j (m t) -> p m j t", t=4)
+            copy(out=target[:, first_run:end_run], in_=source[:, first_run:end_run])
+
+        def first_layer(e, codes, scales):
             acc = psum.tile([P, J, C], F32, name=f"acc1_{e % 2}")
             for t in range(J):
                 channels = slice(t * P, (t + 1) * P)
                 for s in range(PASSES):
+                    slot_codes, slot_scales = slot_operand(e, s)
                     nc.tensor.matmul_mx(
                         out=acc[:, t, :],
-                        lhsT=w1_codes[e][s][:, channels].bitcast(FP8X4),
-                        lhsT_scale=w1_scales[e][s][:, channels],
-                        rhs=slot_codes[s][:, slots].bitcast(FP8X4),
-                        rhs_scale=slot_scales[4 * s : P, slots],
+                        lhsT=codes[:, s, channels].bitcast(FP8X4),
+                        lhsT_scale=scales[:, s, channels],
+                        rhs=slot_codes.bitcast(FP8X4),
+                        rhs_scale=slot_scales,
                         start=(s == 0),
                         stop=(s == PASSES - 1),
                     )
-            hidden = keep.tile([P, C * J], BF16, name=f"hidden_{e}", align_bytes=64)
+            return acc
+
+        def quantise_hidden(acc, hidden):
             nc.scalar.activation(
-                out=hidden[:].rearrange("p (c t) -> p c t", t=J),
+                out=hidden.rearrange("p (c t) -> p c t", t=J),
                 in_=acc[:].rearrange("p t c -> p c t"),
                 func=RELU,
             )
-            codes = keep.tile([P, C], U32, name=f"h_codes_{e}", align_bytes=64)
-            scales = keep.tile([P, C], U8, name=f"h_scales_{e}", align_bytes=64)
-            quantise(hidden, codes[:], scales[:])
-            return codes, scales
+            h_codes = ring.tile([P, C], U32, name="h_codes", align_bytes=64)
+            h_scales = ring.tile([P, C], U8, name="h_scales", align_bytes=64)
+            quantise(hidden, h_codes[:], h_scales[:])
+            return h_codes, h_scales
 
-        def second_layer(e, h, tiles):
-            codes, scales = h
-            acc = psum.tile([P, len(tiles), C], F32, name=f"acc2_{e}_{tiles[0]}")
+        def round_w2(copy, e, grouped, first_column, end_column):
+            copy(
+                out=grouped[:, first_column * J : end_column * J].rearrange("p (c i j) -> p c j i", i=4, j=J),
+                in_=w2_raw[e][:, :, first_column:end_column].rearrange("p j (c i) -> p c j i", i=4),
+            )
+
+        def second_layer(tiles, codes, scales, h_codes, h_scales):
+            acc = psum.tile([P, len(tiles), C], F32, name=f"acc2_{tiles[0]}")
             for i, n in enumerate(tiles):
-                rows = slice(n * P, (n + 1) * P)
                 nc.tensor.matmul_mx(
                     out=acc[:, i, :],
-                    lhsT=w2_codes[e][:, rows].bitcast(FP8X4),
-                    lhsT_scale=w2_scales[e][:, rows],
-                    rhs=codes[:].bitcast(FP8X4),
-                    rhs_scale=scales[:],
+                    lhsT=codes[:, n * P : (n + 1) * P].bitcast(FP8X4),
+                    lhsT_scale=scales[:, n * P : (n + 1) * P],
+                    rhs=h_codes[:].bitcast(FP8X4),
+                    rhs_scale=h_scales[:],
                     start=True,
                     stop=True,
                 )
-            result = keep.tile([P, len(tiles), C], F32, name=f"y_{e}_{tiles[0]}")
-            nc.scalar.copy(out=result[:], in_=acc[:])
+            return acc
+
+        def scatter(e, tiles, acc, y):
+            nc.scalar.copy(out=y, in_=acc[:])
             for i, n in enumerate(tiles):
-                y[(e, n)] = result[:, i, :]
+                nc.vector.tensor_tensor(
+                    windows[n][:].indirect(slot_offsets(e * C, (e + 1) * C)),
+                    y[:, i, :],
+                    gates[:, e * C : (e + 1) * C],
+                    MULT,
+                )
 
-        def scatter(e, n):
-            nc.vector.tensor_tensor(
-                windows[n][:].indirect(offsets[:, e * (C // 16) : (e + 1) * (C // 16)]),
-                y[(e, n)],
-                gates[e][:],
-                MULT,
-            )
+        groups = ((0,), (1, 2), (3,))
+        sums = {}
+        for e in range(E):
+            last = e == E - 1
 
-        for piece in LOADS:
-            load(piece)
+            def earlier(group, y):
+                if e > 0 and groups[group]:
+                    scatter(e - 1, groups[group], sums[group], y[:, : len(groups[group]), 0:C])
 
-        h = {}
-        y = {}
-        waiting = []
-        for piece in LOADS:
-            kind = piece[0]
-            if kind == "xT":
-                s, half = piece[1:]
-                tokens = slice(half * COLS, (half + 1) * COLS)
-                quantise(interleave(piece), x_codes[s][:, tokens], x_scales[4 * s : P, tokens])
-                if half == 1:
-                    nc.vector.tensor_copy(slot_codes[s][:], x_codes[s][:].indirect(offsets[:]))
-                    if s == PASSES - 1:
-                        nc.vector.tensor_copy(slot_scales[:], x_scales[:].indirect(offsets[:]))
-            elif kind == "w1":
-                e, s = piece[1:]
-                quantise(interleave(piece), w1_codes[e][s][:], w1_scales[e][s][:])
-                if s == PASSES - 1:
-                    h[e] = first_layer(e)
-            elif kind == "w2":
-                e, first, columns = piece[1:]
-                rows = slice(first, first + columns)
-                quantise(interleave(piece), w2_codes[e][:, rows], w2_scales[e][:, rows])
-                waiting.append((e, range(first // P, (first + columns) // P)))
-            for e, tiles in list(waiting):
-                if e in h:
-                    second_layer(e, h[e], tiles)
-                    waiting.remove((e, tiles))
-
-        for e in range(E - 1):
-            for n in range(NT):
-                scatter(e, n)
+            grouped = ring.tile([P, PASSES, H * J], BF16, name="w1_grouped", align_bytes=64)
+            codes = ring.tile([P, PASSES, H], U32, name="w1_codes", align_bytes=64)
+            scales = ring.tile([P, PASSES, H], U8, name="w1_scales", align_bytes=64)
+            lead = C // 4
+            cut = P - W1_VECTOR[0]
+            round_w1(nc.scalar.copy, e, 0, grouped, 0, lead)
+            round_w1(nc.scalar.copy, e, 0, grouped, lead, A_CUT)
+            if cut < P:
+                round_w1(nc.vector.tensor_copy, e, 0, grouped, cut, P)
+            earlier(0, w1_raw[e][:, 0])
+            round_w1(nc.scalar.copy, e, 0, grouped, A_CUT, cut)
+            quantise(grouped[:, 0], codes[:, 0], scales[:, 0])
+            cut = P - W1_VECTOR[1]
+            round_w1(nc.scalar.copy, e, 1, grouped, 0, lead)
+            round_w1(nc.scalar.copy, e, 1, grouped, lead, cut)
+            round_w1(nc.vector.tensor_copy, e, 1, grouped, cut, P)
+            parts = 1
+            for part in range(parts):
+                columns = slice(part * H // parts, (part + 1) * H // parts)
+                values = slice(part * H * J // parts, (part + 1) * H * J // parts)
+                quantise(grouped[:, 1, values], codes[:, 1, columns], scales[:, 1, columns])
+            if e == 0:
+                nc.vector.tensor_copy(codes_rest[:], x_codes[1][:].indirect(slot_offsets(C, S)))
+                nc.vector.tensor_copy(scales_rest[:], x_scales[:].indirect(slot_offsets(C, S)))
+            earlier(1, w1_raw[e][:, 1])
+            acc = first_layer(e, codes, scales)
+            grouped = ring.tile([P, N * J], BF16, name="w2_grouped", align_bytes=64)
+            codes = ring.tile([P, N], U32, name="w2_codes", align_bytes=64)
+            scales = ring.tile([P, N], U8, name="w2_scales", align_bytes=64)
+            half_n = N // 2
+            cut = N - 4 * W2_VECTOR
+            if not last:
+                round_w2(nc.scalar.copy, e, grouped, 0, half_n)
+                round_w2(nc.scalar.copy, e, grouped, half_n, cut)
+                if cut < N:
+                    round_w2(nc.vector.tensor_copy, e, grouped, cut, N)
+                quantise(grouped[:], codes[:], scales[:])
+                h_codes, h_scales = quantise_hidden(acc, w2_raw[e][:, 0, 0:half_n].bitcast(BF16))
+                earlier(2, w2_raw[e][:, 1:])
+                for group in range(len(groups)):
+                    if groups[group]:
+                        sums[group] = second_layer(groups[group], codes, scales, h_codes, h_scales)
+            else:
+                round_w2(nc.scalar.copy, e, grouped, 0, half_n)
+                quantise(grouped[:, : half_n * J], codes[:, :half_n], scales[:, :half_n])
+                round_w2(nc.scalar.copy, e, grouped, half_n, 320)
+                h_codes, h_scales = quantise_hidden(acc, w2_raw[e][:, 0, 0:half_n].bitcast(BF16))
+                earlier(2, w2_raw[e][:, 1:])
+                round_w2(nc.scalar.copy, e, grouped, 320, N)
+                quantise(grouped[:, half_n * J :], codes[:, half_n:], scales[:, half_n:])
+                for n in range(NT):
+                    acc = second_layer((n,), codes, scales, h_codes, h_scales)
+                    y = ring.tile([P, 1, C], F32, name=f"y_last{n}")
+                    scatter(e, (n,), acc, y[:])
         for n in range(NT):
             rows = slice(n * P, (n + 1) * P)
-            scatter(E - 1, n)
             for half in range(2):
-                tokens = slice(half * T // 2, (half + 1) * T // 2)
+                tokens = slice(half * half_t, (half + 1) * half_t)
                 nc.vector.tensor_tensor(residual[:, n, tokens], windows[n][:, tokens], residual[:, n, tokens], ADD)
                 nc.sync.dma_start(out=out[rows, tokens], in_=residual[:, n, tokens])

@@ -1,6 +1,7 @@
 from contextlib import ExitStack
 
 import concourse.mybir as mybir
+from concourse.masks import make_identity
 
 K, T, E, C, H, N = 1024, 1024, 4, 128, 512, 512
 S = E * C
@@ -22,10 +23,17 @@ K_PASS = P * J
 PASSES = K // K_PASS
 NT = N // P
 
-X_SCALAR = 44
-W1_VECTOR = (32, 64)
-W2_VECTOR = 0
-A_CUT = 64
+X_SCALAR = 56
+VA = (0,48,32,32)
+VB = (96,80,80,80)
+VC = (48,0,0,0)
+ABS = (16,16,16,16)
+QP = (2,2,2,2)
+C0 = 1
+A_CUT = (80,56,56,56)
+EAGER = (1,1,1,1)
+GROUPS = (((0,),(),(1,2),(3,)),((0,),(),(1,2),(3,)),((0,),(),(1,2),(3,)))
+C_CUT = 320
 
 
 def tile_moe_res_mlp_relu_kernel(tc, xT, xr, w1, w2, gate, offs, out):
@@ -38,15 +46,17 @@ def tile_moe_res_mlp_relu_kernel(tc, xT, xr, w1, w2, gate, offs, out):
         psum = ctx.enter_context(tc.psum_pool(name="psum", bufs=1))
 
         offsets = keep.tile([P, S // 16], U16, name="offsets")
-        gates = keep.tile([P, S], F32, name="gates")
+        gate_first = keep.tile([P, C], F32, name="gate_first")
+        gate_rest = keep.tile([P, S - C], F32, name="gate_rest")
+        identity = keep.tile([P, P], F32, name="identity")
         x_codes = [keep.tile([P, T], U32, name=f"x_codes{s}", align_bytes=64) for s in range(PASSES)]
         x_scales = keep.tile([P, T], U8, name="x_scales", align_bytes=64)
         windows = [keep.tile([P, T], F32, name=f"window{n}") for n in range(NT)]
         x_raw = [big.tile([P, J, T], F32, name="big") for s in range(PASSES)]
         residual = big.tile([P, NT, T], F32, name="big")
-        w1_raw = [first.tile([P, PASSES, J, H], F32, name="w1_raw0", align_bytes=64, offset=0)]
-        w1_raw.extend(keep.tile([P, PASSES, J, H], F32, name=f"w1_raw{e}") for e in range(1, E))
-        w2_raw = [keep.tile([P, J, N], F32, name=f"w2_raw{e}", align_bytes=64) for e in range(E)]
+        w1_raw = [keep.tile([P, PASSES, J, H], F32, name=f"w1_raw{e}") for e in range(E)]
+        w2_raw = [first.tile([P, J, N], F32, name="w2_raw0", align_bytes=64, offset=0)]
+        w2_raw.extend(keep.tile([P, J, N], F32, name=f"w2_raw{e}", align_bytes=64) for e in range(1, E))
 
         table = keep.tile([P, 2], F32, name="table")
         nc.vector.memset(table[:], 0.0)
@@ -54,6 +64,7 @@ def tile_moe_res_mlp_relu_kernel(tc, xT, xr, w1, w2, gate, offs, out):
         nc.gpsimd.memset(x_scales[:], 0)
         for n in range(NT):
             nc.gpsimd.memset(windows[n][:], 0.0)
+        make_identity(nc, identity[:])
 
         def rows_by_four(matrix):
             return matrix.rearrange("(p j) c -> p j c", j=J)
@@ -70,7 +81,9 @@ def tile_moe_res_mlp_relu_kernel(tc, xT, xr, w1, w2, gate, offs, out):
                 nc.sync.dma_start(out=w1_raw[e][:, s], in_=rows_by_four(w1[e][s * K_PASS : (s + 1) * K_PASS, :]))
             nc.sync.dma_start(out=w2_raw[e][:], in_=rows_by_four(w2[e]))
             if e == 0:
-                nc.sync.dma_start(out=gates[:], in_=gate[0:P, :])
+                nc.sync.dma_start(out=gate_first[:], in_=gate[0:P, :C])
+            if e == 1:
+                nc.sync.dma_start(out=gate_rest[:], in_=gate[0:P, C:])
         for n in range(NT):
             nc.sync.dma_start(out=residual[:, n, :], in_=xr[n * P : (n + 1) * P, :])
 
@@ -81,8 +94,7 @@ def tile_moe_res_mlp_relu_kernel(tc, xT, xr, w1, w2, gate, offs, out):
             return offsets[:, first_slot // 16 : end_slot // 16]
 
         half_t = T // 2
-        codes_pass0 = keep.tile([P, S], U32, name="codes_pass0", align_bytes=64)
-        codes_first = keep.tile([P, C], U32, name="codes_first", align_bytes=64)
+        slot_codes = [keep.tile([P, S], U32, name=f"slot_codes{s}", align_bytes=64) for s in range(PASSES)]
         scales_first = keep.tile([P, C], U8, name="scales_first", align_bytes=64)
         for s in range(PASSES):
             for half in range(2):
@@ -93,41 +105,35 @@ def tile_moe_res_mlp_relu_kernel(tc, xT, xr, w1, w2, gate, offs, out):
                 nc.scalar.copy(out=target[:, :X_SCALAR], in_=source[:, :X_SCALAR])
                 nc.vector.tensor_copy(out=target[:, X_SCALAR:], in_=source[:, X_SCALAR:])
                 quantise(grouped[:], x_codes[s][:, tokens], x_scales[4 * s : P, tokens])
-            if s == 0:
-                nc.vector.tensor_copy(codes_pass0[:], x_codes[0][:].indirect(offsets[:]))
-        nc.vector.tensor_copy(codes_first[:], x_codes[1][:].indirect(slot_offsets(0, C)))
+            nc.vector.tensor_copy(slot_codes[s][:], x_codes[s][:].indirect(offsets[:]))
         nc.vector.tensor_copy(scales_first[:], x_scales[:].indirect(slot_offsets(0, C)))
-        codes_rest = first.tile([P, S - C], U32, name="codes_rest", align_bytes=64, offset=0)
-        scales_rest = first.tile([P, S - C], U8, name="scales_rest", align_bytes=64, offset=(S - C) * 4)
+        scales_rest = first.tile([P, S - C], U8, name="scales_rest", align_bytes=64, offset=0)
 
         def slot_operand(e, s):
             if e == 0:
-                codes = codes_first[:]
                 scales = scales_first[4 * s : P, :]
             else:
-                codes = codes_rest[:, (e - 1) * C : e * C]
                 scales = scales_rest[4 * s : P, (e - 1) * C : e * C]
-            if s == 0:
-                codes = codes_pass0[:, e * C : (e + 1) * C]
-            return codes, scales
+            return slot_codes[s][:, e * C : (e + 1) * C], scales
 
         def round_w1(copy, e, s, grouped, first_run, end_run):
-            target = grouped[:, s].rearrange("p (t m j) -> p m j t", t=4, j=J)
-            source = w1_raw[e][:, s].rearrange("p j (m t) -> p m j t", t=4)
-            copy(out=target[:, first_run:end_run], in_=source[:, first_run:end_run])
+            target = grouped[:].rearrange("p s (t m j) -> p s m j t", t=4, j=J)
+            source = w1_raw[e][:].rearrange("p s j (m t) -> p s m j t", t=4)
+            if end_run > first_run:
+                copy(out=target[:, s, first_run:end_run], in_=source[:, s, first_run:end_run])
 
         def first_layer(e, codes, scales):
             acc = psum.tile([P, J, C], F32, name=f"acc1_{e % 2}")
             for t in range(J):
                 channels = slice(t * P, (t + 1) * P)
                 for s in range(PASSES):
-                    slot_codes, slot_scales = slot_operand(e, s)
+                    x_words, x_bytes = slot_operand(e, s)
                     nc.tensor.matmul_mx(
                         out=acc[:, t, :],
                         lhsT=codes[:, s, channels].bitcast(FP8X4),
                         lhsT_scale=scales[:, s, channels],
-                        rhs=slot_codes.bitcast(FP8X4),
-                        rhs_scale=slot_scales,
+                        rhs=x_words.bitcast(FP8X4),
+                        rhs_scale=x_bytes,
                         start=(s == 0),
                         stop=(s == PASSES - 1),
                     )
@@ -170,76 +176,137 @@ def tile_moe_res_mlp_relu_kernel(tc, xT, xr, w1, w2, gate, offs, out):
                 nc.vector.tensor_tensor(
                     windows[n][:].indirect(slot_offsets(e * C, (e + 1) * C)),
                     y[:, i, :],
-                    gates[:, e * C : (e + 1) * C],
+                    gate_first[:] if e == 0 else gate_rest[:, (e - 1) * C : e * C],
                     MULT,
                 )
 
-        groups = ((0,), (1, 2), (3,))
+        def finish(n, first_token, end_token):
+            tokens = slice(first_token, end_token)
+            nc.vector.tensor_tensor(residual[:, n, tokens], windows[n][:, tokens], residual[:, n, tokens], ADD)
+            nc.sync.dma_start(out=out[n * P : (n + 1) * P, tokens], in_=residual[:, n, tokens])
+
+        def finish_on_tensor(n):
+            rows = slice(n * P, (n + 1) * P)
+            banks = [psum.tile([P, J, P], F32, name=f"turned{half}") for half in range(2)]
+            for source, opens in ((residual[:, n], True), (windows[n][:], False)):
+                for half in range(2):
+                    for b in range(J):
+                        first_token = half * half_t + b * P
+                        nc.tensor.matmul(
+                            banks[half][:, b, :],
+                            source[:, first_token : first_token + P],
+                            identity[:],
+                            is_transpose=True,
+                            start=(opens and b == 0),
+                            stop=(not opens and b == J - 1),
+                        )
+            for half in range(2):
+                turned = ring.tile([P, J, P], F32, name="turned_sum")
+                nc.scalar.copy(out=turned[:], in_=banks[half][:])
+                back = psum.tile([P, J, P], F32, name=f"acc1_{half}")
+                for b in range(J):
+                    nc.tensor.transpose(back[:, b, :], turned[:, b, :], identity[:])
+                result = ring.tile([P, J, P], F32, name="result")
+                nc.scalar.copy(out=result[:], in_=back[:])
+                nc.scalar.dma_start(
+                    out=out[rows, half * half_t : (half + 1) * half_t], in_=result[:].rearrange("p b c -> p (b c)")
+                )
+
         sums = {}
         for e in range(E):
             last = e == E - 1
 
             def earlier(group, y):
-                if e > 0 and groups[group]:
-                    scatter(e - 1, groups[group], sums[group], y[:, : len(groups[group]), 0:C])
+                if e > 0 and GROUPS[e - 1][group]:
+                    tiles = GROUPS[e - 1][group]
+                    scatter(e - 1, tiles, sums[group], y[:, : len(tiles), 0:C])
 
             grouped = ring.tile([P, PASSES, H * J], BF16, name="w1_grouped", align_bytes=64)
             codes = ring.tile([P, PASSES, H], U32, name="w1_codes", align_bytes=64)
             scales = ring.tile([P, PASSES, H], U8, name="w1_scales", align_bytes=64)
             lead = C // 4
-            cut = P - W1_VECTOR[0]
-            round_w1(nc.scalar.copy, e, 0, grouped, 0, lead)
-            round_w1(nc.scalar.copy, e, 0, grouped, lead, A_CUT)
-            if cut < P:
-                round_w1(nc.vector.tensor_copy, e, 0, grouped, cut, P)
-            earlier(0, w1_raw[e][:, 0])
-            round_w1(nc.scalar.copy, e, 0, grouped, A_CUT, cut)
-            quantise(grouped[:, 0], codes[:, 0], scales[:, 0])
-            cut = P - W1_VECTOR[1]
-            round_w1(nc.scalar.copy, e, 1, grouped, 0, lead)
+            AB = ABS[e]
+            cut = P - VA[e]
+            round_w1(nc.scalar.copy, e, 0, grouped, AB, AB + lead)
+            a_cut = min(A_CUT[e], cut)
+            round_w1(nc.scalar.copy, e, 0, grouped, AB + lead, a_cut)
+            round_w1(nc.vector.tensor_copy, e, 0, grouped, cut, P)
+            earlier(1, w1_raw[e][:, 0, :, 4 * AB :])
+            round_w1(nc.scalar.copy, e, 0, grouped, a_cut, cut)
+            if AB == 0:
+                quantise(grouped[:, 0], codes[:, 0], scales[:, 0])
+            cut = P - VB[e]
+            round_w1(nc.scalar.copy, e, slice(0, 2), grouped, 0, AB)
+            round_w1(nc.scalar.copy, e, 1, grouped, AB, lead)
             round_w1(nc.scalar.copy, e, 1, grouped, lead, cut)
             round_w1(nc.vector.tensor_copy, e, 1, grouped, cut, P)
-            parts = 1
+            parts = QP[e]
             for part in range(parts):
-                columns = slice(part * H // parts, (part + 1) * H // parts)
-                values = slice(part * H * J // parts, (part + 1) * H * J // parts)
-                quantise(grouped[:, 1, values], codes[:, 1, columns], scales[:, 1, columns])
-            if e == 0:
-                nc.vector.tensor_copy(codes_rest[:], x_codes[1][:].indirect(slot_offsets(C, S)))
-                nc.vector.tensor_copy(scales_rest[:], x_scales[:].indirect(slot_offsets(C, S)))
-            earlier(1, w1_raw[e][:, 1])
+                for s in range(0 if AB else 1, PASSES):
+                    columns = slice(part * H // parts, (part + 1) * H // parts)
+                    values = slice(part * H * J // parts, (part + 1) * H * J // parts)
+                    quantise(grouped[:, s, values], codes[:, s, columns], scales[:, s, columns])
+            earlier(2, w1_raw[e][:, 1])
             acc = first_layer(e, codes, scales)
             grouped = ring.tile([P, N * J], BF16, name="w2_grouped", align_bytes=64)
             codes = ring.tile([P, N], U32, name="w2_codes", align_bytes=64)
             scales = ring.tile([P, N], U8, name="w2_scales", align_bytes=64)
             half_n = N // 2
-            cut = N - 4 * W2_VECTOR
-            if not last:
+            cut = N - 4 * VC[e]
+            if EAGER[e] == 2:
+                for q in range(C0):
+                    round_w2(nc.scalar.copy, e, grouped, q * P, (q + 1) * P)
+                    quantise(grouped[:, q * P * J : (q + 1) * P * J], codes[:, q * P : (q + 1) * P], scales[:, q * P : (q + 1) * P])
+                hidden = ring.tile([P, C * J], BF16, name="hidden", align_bytes=64)
+                h_codes, h_scales = quantise_hidden(acc, hidden[:])
+                earlier(3, w2_raw[e][:, 1:])
+                for q in range(C0, NT):
+                    round_w2(nc.scalar.copy, e, grouped, q * P, (q + 1) * P)
+                    quantise(grouped[:, q * P * J : (q + 1) * P * J], codes[:, q * P : (q + 1) * P], scales[:, q * P : (q + 1) * P])
+            else:
                 round_w2(nc.scalar.copy, e, grouped, 0, half_n)
+            if EAGER[e] == 2:
+                pass
+            elif not EAGER[e]:
                 round_w2(nc.scalar.copy, e, grouped, half_n, cut)
                 if cut < N:
                     round_w2(nc.vector.tensor_copy, e, grouped, cut, N)
                 quantise(grouped[:], codes[:], scales[:])
                 h_codes, h_scales = quantise_hidden(acc, w2_raw[e][:, 0, 0:half_n].bitcast(BF16))
-                earlier(2, w2_raw[e][:, 1:])
-                for group in range(len(groups)):
-                    if groups[group]:
-                        sums[group] = second_layer(groups[group], codes, scales, h_codes, h_scales)
+                earlier(3, w2_raw[e][:, 1:])
             else:
-                round_w2(nc.scalar.copy, e, grouped, 0, half_n)
                 quantise(grouped[:, : half_n * J], codes[:, :half_n], scales[:, :half_n])
-                round_w2(nc.scalar.copy, e, grouped, half_n, 320)
+                if C_CUT > half_n:
+                    round_w2(nc.scalar.copy, e, grouped, half_n, C_CUT)
                 h_codes, h_scales = quantise_hidden(acc, w2_raw[e][:, 0, 0:half_n].bitcast(BF16))
-                earlier(2, w2_raw[e][:, 1:])
-                round_w2(nc.scalar.copy, e, grouped, 320, N)
+                earlier(3, w2_raw[e][:, 1:])
+                if cut > C_CUT:
+                    round_w2(nc.scalar.copy, e, grouped, C_CUT, cut)
+                if cut < N:
+                    round_w2(nc.vector.tensor_copy, e, grouped, cut, N)
                 quantise(grouped[:, half_n * J :], codes[:, half_n:], scales[:, half_n:])
+            if e == 0:
+                nc.vector.tensor_copy(scales_rest[:], x_scales[:].indirect(slot_offsets(C, S)))
+            if not last:
+                for group in range(4):
+                    if GROUPS[e][group]:
+                        sums[group] = second_layer(GROUPS[e][group], codes, scales, h_codes, h_scales)
+                if GROUPS[e][0]:
+                    y = ring.tile([P, len(GROUPS[e][0]), C], F32, name=f"y_now{e}")
+                    scatter(e, GROUPS[e][0], sums[0], y[:])
+            else:
                 for n in range(NT):
                     acc = second_layer((n,), codes, scales, h_codes, h_scales)
                     y = ring.tile([P, 1, C], F32, name=f"y_last{n}")
                     scatter(e, (n,), acc, y[:])
-        for n in range(NT):
-            rows = slice(n * P, (n + 1) * P)
-            for half in range(2):
-                tokens = slice(half * half_t, (half + 1) * half_t)
-                nc.vector.tensor_tensor(residual[:, n, tokens], windows[n][:, tokens], residual[:, n, tokens], ADD)
-                nc.sync.dma_start(out=out[rows, tokens], in_=residual[:, n, tokens])
+                    if n == 0:
+                        finish_on_tensor(0)
+                    if n == 2:
+                        finish(1, 0, half_t)
+                        finish(1, half_t, T)
+                    if n == 3:
+                        finish(2, 0, half_t)
+                        finish(2, half_t, T)
+                        finish(3, 0, half_t)
+                        finish(3, half_t, 3 * T // 4)
+                        finish(3, 3 * T // 4, T)

@@ -22,18 +22,16 @@ J = 4
 K_PASS = P * J
 PASSES = K // K_PASS
 NT = N // P
+HALF_T = T // 2
+HALF_N = N // 2
+RUNS = H // 4
+SLOT_RUNS = C // 4
 
-X_SCALAR = 56
-VA = (0,48,32,32)
-VB = (96,80,80,80)
-VC = (48,0,0,0)
-ABS = (16,16,16,16)
-QP = (2,2,2,2)
-C0 = 1
-A_CUT = (80,56,56,56)
-EAGER = (1,1,1,1)
-GROUPS = (((0,),(),(1,2),(3,)),((0,),(),(1,2),(3,)),((0,),(),(1,2),(3,)))
-C_CUT = 320
+X_SCALAR_RUNS = 56
+W1_VECTOR_RUNS = ((40, 80), (40, 80), (40, 80), (40, 80))
+JOINT_RUNS = 16
+W2_BEFORE_RELU = 320
+W2_VECTOR_FIRST = 192
 
 
 def tile_moe_res_mlp_relu_kernel(tc, xT, xr, w1, w2, gate, offs, out):
@@ -46,21 +44,25 @@ def tile_moe_res_mlp_relu_kernel(tc, xT, xr, w1, w2, gate, offs, out):
         psum = ctx.enter_context(tc.psum_pool(name="psum", bufs=1))
 
         offsets = keep.tile([P, S // 16], U16, name="offsets")
-        gate_first = keep.tile([P, C], F32, name="gate_first")
-        gate_rest = keep.tile([P, S - C], F32, name="gate_rest")
+        gate_rows = keep.tile([P, C], F32, name="gate_rows")
+        gate_columns = keep.tile([P, E], F32, name="gate_columns")
+        gates = keep.tile([P, E, C], F32, name="gates")
         identity = keep.tile([P, P], F32, name="identity")
         x_codes = [keep.tile([P, T], U32, name=f"x_codes{s}", align_bytes=64) for s in range(PASSES)]
         x_scales = keep.tile([P, T], U8, name="x_scales", align_bytes=64)
         windows = [keep.tile([P, T], F32, name=f"window{n}") for n in range(NT)]
         x_raw = [big.tile([P, J, T], F32, name="big") for s in range(PASSES)]
         residual = big.tile([P, NT, T], F32, name="big")
-        w1_raw = [keep.tile([P, PASSES, J, H], F32, name=f"w1_raw{e}") for e in range(E)]
-        w2_raw = [first.tile([P, J, N], F32, name="w2_raw0", align_bytes=64, offset=0)]
+        w1_bytes = PASSES * J * H * 4
+        w1_raw = [first.tile([P, PASSES, J, H], F32, name="w1_raw0", align_bytes=64, offset=0)]
+        w1_raw.extend(keep.tile([P, PASSES, J, H], F32, name=f"w1_raw{e}") for e in range(1, E))
+        w2_raw = [first.tile([P, J, N], F32, name="w2_raw0", align_bytes=64, offset=w1_bytes)]
         w2_raw.extend(keep.tile([P, J, N], F32, name=f"w2_raw{e}", align_bytes=64) for e in range(1, E))
 
         table = keep.tile([P, 2], F32, name="table")
         nc.vector.memset(table[:], 0.0)
         nc.scalar.activation(out=table[:, 1:2], in_=table[:, 0:1], func=RELU)
+        nc.vector.memset(gate_rows[:], 0.0)
         nc.gpsimd.memset(x_scales[:], 0)
         for n in range(NT):
             nc.gpsimd.memset(windows[n][:], 0.0)
@@ -70,22 +72,24 @@ def tile_moe_res_mlp_relu_kernel(tc, xT, xr, w1, w2, gate, offs, out):
             return matrix.rearrange("(p j) c -> p j c", j=J)
 
         for s in range(PASSES):
-            source = rows_by_four(xT[s * K_PASS : (s + 1) * K_PASS, :])
-            for half in range(2):
-                rows = slice(2 * half, 2 * half + 2)
-                nc.sync.dma_start(out=x_raw[s][:, rows, :], in_=source[:, rows, :])
+            nc.sync.dma_start(out=x_raw[s][:], in_=rows_by_four(xT[s * K_PASS : (s + 1) * K_PASS, :]))
             if s == 0:
                 nc.sync.dma_start(offsets[:], offs)
+                nc.sync.dma_start(out=gate_rows[0:E, :], in_=gate[0:1, :].rearrange("r (e c) -> (r e) c", e=E))
         for e in range(E):
             for s in range(PASSES):
                 nc.sync.dma_start(out=w1_raw[e][:, s], in_=rows_by_four(w1[e][s * K_PASS : (s + 1) * K_PASS, :]))
             nc.sync.dma_start(out=w2_raw[e][:], in_=rows_by_four(w2[e]))
-            if e == 0:
-                nc.sync.dma_start(out=gate_first[:], in_=gate[0:P, :C])
-            if e == 1:
-                nc.sync.dma_start(out=gate_rest[:], in_=gate[0:P, C:])
         for n in range(NT):
             nc.sync.dma_start(out=residual[:, n, :], in_=xr[n * P : (n + 1) * P, :])
+
+        turned_gate = psum.tile([P, P], F32, name="turned_sums0")
+        nc.tensor.transpose(turned_gate[:], gate_rows[:], identity[:])
+        nc.scalar.copy(out=gate_columns[:], in_=turned_gate[:, 0:E])
+        spread_gate = psum.tile([P, E, C], F32, name="turned_sums1")
+        for e in range(E):
+            nc.tensor.transpose(spread_gate[:, e, :], gate_columns[:, e : e + 1].to_broadcast([P, P]), identity[:])
+        nc.scalar.copy(out=gates[:], in_=spread_gate[:])
 
         def quantise(grouped, codes, scales):
             nc.vector.quantize_mx(out=codes.bitcast(FP8X4), scales=scales, in_=grouped)
@@ -93,37 +97,62 @@ def tile_moe_res_mlp_relu_kernel(tc, xT, xr, w1, w2, gate, offs, out):
         def slot_offsets(first_slot, end_slot):
             return offsets[:, first_slot // 16 : end_slot // 16]
 
-        half_t = T // 2
-        slot_codes = [keep.tile([P, S], U32, name=f"slot_codes{s}", align_bytes=64) for s in range(PASSES)]
-        scales_first = keep.tile([P, C], U8, name="scales_first", align_bytes=64)
         for s in range(PASSES):
             for half in range(2):
-                tokens = slice(half * half_t, (half + 1) * half_t)
-                grouped = ring.tile([P, half_t * J], BF16, name="x_grouped", align_bytes=64)
+                tokens = slice(half * HALF_T, (half + 1) * HALF_T)
+                grouped = ring.tile([P, HALF_T * J], BF16, name="x_grouped", align_bytes=64)
                 target = grouped[:].rearrange("p (c i j) -> p c j i", i=4, j=J)
                 source = x_raw[s][:, :, tokens].rearrange("p j (c i) -> p c j i", i=4)
-                nc.scalar.copy(out=target[:, :X_SCALAR], in_=source[:, :X_SCALAR])
-                nc.vector.tensor_copy(out=target[:, X_SCALAR:], in_=source[:, X_SCALAR:])
+                nc.scalar.copy(out=target[:, :X_SCALAR_RUNS], in_=source[:, :X_SCALAR_RUNS])
+                nc.vector.tensor_copy(out=target[:, X_SCALAR_RUNS:], in_=source[:, X_SCALAR_RUNS:])
                 quantise(grouped[:], x_codes[s][:, tokens], x_scales[4 * s : P, tokens])
-            nc.vector.tensor_copy(slot_codes[s][:], x_codes[s][:].indirect(offsets[:]))
+            if s == 0:
+                codes_pass0 = keep.tile([P, S], U32, name="codes_pass0", align_bytes=64)
+                nc.vector.tensor_copy(codes_pass0[:], x_codes[0][:].indirect(offsets[:]))
+        codes_first = keep.tile([P, S], U32, name="codes_first", align_bytes=64)
+        scales_first = keep.tile([P, C], U8, name="scales_first", align_bytes=64)
+        nc.vector.tensor_copy(codes_first[:], x_codes[1][:].indirect(slot_offsets(0, S)))
         nc.vector.tensor_copy(scales_first[:], x_scales[:].indirect(slot_offsets(0, C)))
-        scales_rest = first.tile([P, S - C], U8, name="scales_rest", align_bytes=64, offset=0)
+        scales_rest = first.tile([P, S - C], U8, name="scales_rest", align_bytes=64, offset=w1_bytes)
 
         def slot_operand(e, s):
-            if e == 0:
-                scales = scales_first[4 * s : P, :]
+            rest = slice((e - 1) * C, e * C)
+            if s == 0:
+                codes = codes_pass0[:, e * C : (e + 1) * C]
             else:
-                scales = scales_rest[4 * s : P, (e - 1) * C : e * C]
-            return slot_codes[s][:, e * C : (e + 1) * C], scales
+                codes = codes_first[:, e * C : (e + 1) * C]
+            scales = scales_first[4 * s : P, :] if e == 0 else scales_rest[4 * s : P, rest]
+            return codes, scales
 
-        def round_w1(copy, e, s, grouped, first_run, end_run):
+        def quantise_w1(e):
+            grouped = ring.tile([P, PASSES, H * J], BF16, name="w1_grouped", align_bytes=64)
             target = grouped[:].rearrange("p s (t m j) -> p s m j t", t=4, j=J)
             source = w1_raw[e][:].rearrange("p s j (m t) -> p s m j t", t=4)
-            if end_run > first_run:
-                copy(out=target[:, s, first_run:end_run], in_=source[:, s, first_run:end_run])
+
+            def rounded(copy, passes, first_run, end_run):
+                copy(out=target[:, passes, first_run:end_run], in_=source[:, passes, first_run:end_run])
+
+            cuts = [RUNS - runs for runs in W1_VECTOR_RUNS[e]]
+            rounded(nc.scalar.copy, 0, JOINT_RUNS, JOINT_RUNS + SLOT_RUNS)
+            rounded(nc.scalar.copy, 0, JOINT_RUNS + SLOT_RUNS, cuts[0])
+            if cuts[0] < RUNS:
+                rounded(nc.vector.tensor_copy, 0, cuts[0], RUNS)
+            rounded(nc.scalar.copy, slice(0, PASSES), 0, JOINT_RUNS)
+            rounded(nc.scalar.copy, 1, JOINT_RUNS, SLOT_RUNS)
+            if cuts[1] > SLOT_RUNS:
+                rounded(nc.scalar.copy, 1, SLOT_RUNS, cuts[1])
+            rounded(nc.vector.tensor_copy, 1, cuts[1], RUNS)
+            codes = ring.tile([P, PASSES, H], U32, name="w1_codes", align_bytes=64)
+            scales = ring.tile([P, PASSES, H], U8, name="w1_scales", align_bytes=64)
+            for half in range(2):
+                for s in range(PASSES):
+                    columns = slice(half * H // 2, (half + 1) * H // 2)
+                    values = slice(half * H * J // 2, (half + 1) * H * J // 2)
+                    quantise(grouped[:, s, values], codes[:, s, columns], scales[:, s, columns])
+            return codes, scales
 
         def first_layer(e, codes, scales):
-            acc = psum.tile([P, J, C], F32, name=f"acc1_{e % 2}")
+            acc = psum.tile([P, J, C], F32, name=f"hidden_sums{e % 2}")
             for t in range(J):
                 channels = slice(t * P, (t + 1) * P)
                 for s in range(PASSES):
@@ -139,7 +168,8 @@ def tile_moe_res_mlp_relu_kernel(tc, xT, xr, w1, w2, gate, offs, out):
                     )
             return acc
 
-        def quantise_hidden(acc, hidden):
+        def quantise_hidden(e, acc):
+            hidden = w2_raw[e][:, 0, 0:HALF_N].bitcast(BF16)
             nc.scalar.activation(
                 out=hidden.rearrange("p (c t) -> p c t", t=J),
                 in_=acc[:].rearrange("p t c -> p c t"),
@@ -157,7 +187,7 @@ def tile_moe_res_mlp_relu_kernel(tc, xT, xr, w1, w2, gate, offs, out):
             )
 
         def second_layer(tiles, codes, scales, h_codes, h_scales):
-            acc = psum.tile([P, len(tiles), C], F32, name=f"acc2_{tiles[0]}")
+            acc = psum.tile([P, len(tiles), C], F32, name=f"result_sums{tiles[0]}")
             for i, n in enumerate(tiles):
                 nc.tensor.matmul_mx(
                     out=acc[:, i, :],
@@ -174,24 +204,20 @@ def tile_moe_res_mlp_relu_kernel(tc, xT, xr, w1, w2, gate, offs, out):
             nc.scalar.copy(out=y, in_=acc[:])
             for i, n in enumerate(tiles):
                 nc.vector.tensor_tensor(
-                    windows[n][:].indirect(slot_offsets(e * C, (e + 1) * C)),
-                    y[:, i, :],
-                    gate_first[:] if e == 0 else gate_rest[:, (e - 1) * C : e * C],
-                    MULT,
+                    windows[n][:].indirect(slot_offsets(e * C, (e + 1) * C)), y[:, i, :], gates[:, e, :], MULT
                 )
 
-        def finish(n, first_token, end_token):
+        def finish_on_vector(n, first_token, end_token):
             tokens = slice(first_token, end_token)
             nc.vector.tensor_tensor(residual[:, n, tokens], windows[n][:, tokens], residual[:, n, tokens], ADD)
             nc.sync.dma_start(out=out[n * P : (n + 1) * P, tokens], in_=residual[:, n, tokens])
 
         def finish_on_tensor(n):
-            rows = slice(n * P, (n + 1) * P)
-            banks = [psum.tile([P, J, P], F32, name=f"turned{half}") for half in range(2)]
+            banks = [psum.tile([P, J, P], F32, name=f"turned_sums{half}") for half in range(2)]
             for source, opens in ((residual[:, n], True), (windows[n][:], False)):
                 for half in range(2):
                     for b in range(J):
-                        first_token = half * half_t + b * P
+                        first_token = half * HALF_T + b * P
                         nc.tensor.matmul(
                             banks[half][:, b, :],
                             source[:, first_token : first_token + P],
@@ -201,112 +227,55 @@ def tile_moe_res_mlp_relu_kernel(tc, xT, xr, w1, w2, gate, offs, out):
                             stop=(not opens and b == J - 1),
                         )
             for half in range(2):
-                turned = ring.tile([P, J, P], F32, name="turned_sum")
+                turned = ring.tile([P, J, P], F32, name="turned")
                 nc.scalar.copy(out=turned[:], in_=banks[half][:])
-                back = psum.tile([P, J, P], F32, name=f"acc1_{half}")
+                back = psum.tile([P, J, P], F32, name=f"hidden_sums{half}")
                 for b in range(J):
                     nc.tensor.transpose(back[:, b, :], turned[:, b, :], identity[:])
-                result = ring.tile([P, J, P], F32, name="result")
-                nc.scalar.copy(out=result[:], in_=back[:])
-                nc.scalar.dma_start(
-                    out=out[rows, half * half_t : (half + 1) * half_t], in_=result[:].rearrange("p b c -> p (b c)")
-                )
+                result = ring.tile([P, HALF_T], F32, name="result")
+                nc.scalar.copy(out=result[:], in_=back[:].rearrange("p b c -> p (b c)"))
+                nc.scalar.dma_start(out=out[n * P : (n + 1) * P, half * HALF_T : (half + 1) * HALF_T], in_=result[:])
 
-        sums = {}
+        groups = (((0,), (1, 2), (3,)), ((0,), (1, 2), (3,)), ((0,), (1, 2), (3,)))
+        sums = []
         for e in range(E):
-            last = e == E - 1
-
-            def earlier(group, y):
-                if e > 0 and GROUPS[e - 1][group]:
-                    tiles = GROUPS[e - 1][group]
-                    scatter(e - 1, tiles, sums[group], y[:, : len(tiles), 0:C])
-
-            grouped = ring.tile([P, PASSES, H * J], BF16, name="w1_grouped", align_bytes=64)
-            codes = ring.tile([P, PASSES, H], U32, name="w1_codes", align_bytes=64)
-            scales = ring.tile([P, PASSES, H], U8, name="w1_scales", align_bytes=64)
-            lead = C // 4
-            AB = ABS[e]
-            cut = P - VA[e]
-            round_w1(nc.scalar.copy, e, 0, grouped, AB, AB + lead)
-            a_cut = min(A_CUT[e], cut)
-            round_w1(nc.scalar.copy, e, 0, grouped, AB + lead, a_cut)
-            round_w1(nc.vector.tensor_copy, e, 0, grouped, cut, P)
-            earlier(1, w1_raw[e][:, 0, :, 4 * AB :])
-            round_w1(nc.scalar.copy, e, 0, grouped, a_cut, cut)
-            if AB == 0:
-                quantise(grouped[:, 0], codes[:, 0], scales[:, 0])
-            cut = P - VB[e]
-            round_w1(nc.scalar.copy, e, slice(0, 2), grouped, 0, AB)
-            round_w1(nc.scalar.copy, e, 1, grouped, AB, lead)
-            round_w1(nc.scalar.copy, e, 1, grouped, lead, cut)
-            round_w1(nc.vector.tensor_copy, e, 1, grouped, cut, P)
-            parts = QP[e]
-            for part in range(parts):
-                for s in range(0 if AB else 1, PASSES):
-                    columns = slice(part * H // parts, (part + 1) * H // parts)
-                    values = slice(part * H * J // parts, (part + 1) * H * J // parts)
-                    quantise(grouped[:, s, values], codes[:, s, columns], scales[:, s, columns])
-            earlier(2, w1_raw[e][:, 1])
+            codes, scales = quantise_w1(e)
+            if e > 0:
+                tiles = groups[e - 1][1]
+                scatter(e - 1, tiles, sums[1], w1_raw[e][:, 1, 0 : len(tiles), 0:C])
             acc = first_layer(e, codes, scales)
             grouped = ring.tile([P, N * J], BF16, name="w2_grouped", align_bytes=64)
             codes = ring.tile([P, N], U32, name="w2_codes", align_bytes=64)
             scales = ring.tile([P, N], U8, name="w2_scales", align_bytes=64)
-            half_n = N // 2
-            cut = N - 4 * VC[e]
-            if EAGER[e] == 2:
-                for q in range(C0):
-                    round_w2(nc.scalar.copy, e, grouped, q * P, (q + 1) * P)
-                    quantise(grouped[:, q * P * J : (q + 1) * P * J], codes[:, q * P : (q + 1) * P], scales[:, q * P : (q + 1) * P])
-                hidden = ring.tile([P, C * J], BF16, name="hidden", align_bytes=64)
-                h_codes, h_scales = quantise_hidden(acc, hidden[:])
-                earlier(3, w2_raw[e][:, 1:])
-                for q in range(C0, NT):
-                    round_w2(nc.scalar.copy, e, grouped, q * P, (q + 1) * P)
-                    quantise(grouped[:, q * P * J : (q + 1) * P * J], codes[:, q * P : (q + 1) * P], scales[:, q * P : (q + 1) * P])
-            else:
-                round_w2(nc.scalar.copy, e, grouped, 0, half_n)
-            if EAGER[e] == 2:
-                pass
-            elif not EAGER[e]:
-                round_w2(nc.scalar.copy, e, grouped, half_n, cut)
-                if cut < N:
-                    round_w2(nc.vector.tensor_copy, e, grouped, cut, N)
-                quantise(grouped[:], codes[:], scales[:])
-                h_codes, h_scales = quantise_hidden(acc, w2_raw[e][:, 0, 0:half_n].bitcast(BF16))
-                earlier(3, w2_raw[e][:, 1:])
-            else:
-                quantise(grouped[:, : half_n * J], codes[:, :half_n], scales[:, :half_n])
-                if C_CUT > half_n:
-                    round_w2(nc.scalar.copy, e, grouped, half_n, C_CUT)
-                h_codes, h_scales = quantise_hidden(acc, w2_raw[e][:, 0, 0:half_n].bitcast(BF16))
-                earlier(3, w2_raw[e][:, 1:])
-                if cut > C_CUT:
-                    round_w2(nc.scalar.copy, e, grouped, C_CUT, cut)
-                if cut < N:
-                    round_w2(nc.vector.tensor_copy, e, grouped, cut, N)
-                quantise(grouped[:, half_n * J :], codes[:, half_n:], scales[:, half_n:])
+            round_w2(nc.scalar.copy, e, grouped, 0, HALF_N)
+            quantise(grouped[:, : HALF_N * J], codes[:, :HALF_N], scales[:, :HALF_N])
+            before = W2_BEFORE_RELU
+            if before > HALF_N:
+                round_w2(nc.scalar.copy, e, grouped, HALF_N, before)
+            h_codes, h_scales = quantise_hidden(e, acc)
+            if e > 0 and len(groups[e - 1]) > 2:
+                scatter(e - 1, groups[e - 1][2], sums[2], w2_raw[e][:, 1:2, 0:C])
+            cut = N - (W2_VECTOR_FIRST if e == 0 else 0)
+            if cut > before:
+                round_w2(nc.scalar.copy, e, grouped, before, cut)
+            if cut < N:
+                round_w2(nc.vector.tensor_copy, e, grouped, cut, N)
+            quantise(grouped[:, HALF_N * J :], codes[:, HALF_N:], scales[:, HALF_N:])
             if e == 0:
                 nc.vector.tensor_copy(scales_rest[:], x_scales[:].indirect(slot_offsets(C, S)))
-            if not last:
-                for group in range(4):
-                    if GROUPS[e][group]:
-                        sums[group] = second_layer(GROUPS[e][group], codes, scales, h_codes, h_scales)
-                if GROUPS[e][0]:
-                    y = ring.tile([P, len(GROUPS[e][0]), C], F32, name=f"y_now{e}")
-                    scatter(e, GROUPS[e][0], sums[0], y[:])
-            else:
-                for n in range(NT):
-                    acc = second_layer((n,), codes, scales, h_codes, h_scales)
-                    y = ring.tile([P, 1, C], F32, name=f"y_last{n}")
-                    scatter(e, (n,), acc, y[:])
-                    if n == 0:
-                        finish_on_tensor(0)
-                    if n == 2:
-                        finish(1, 0, half_t)
-                        finish(1, half_t, T)
-                    if n == 3:
-                        finish(2, 0, half_t)
-                        finish(2, half_t, T)
-                        finish(3, 0, half_t)
-                        finish(3, half_t, 3 * T // 4)
-                        finish(3, 3 * T // 4, T)
+            if e < E - 1:
+                sums = [second_layer(tiles, codes, scales, h_codes, h_scales) for tiles in groups[e]]
+                y = ring.tile([P, len(groups[e][0]), C], F32, name=f"y_first{e}")
+                scatter(e, groups[e][0], sums[0], y[:])
+        for n in range(NT):
+            acc = second_layer((n,), codes, scales, h_codes, h_scales)
+            y = ring.tile([P, 1, C], F32, name=f"y_last{n}")
+            scatter(E - 1, (n,), acc, y[:])
+            if n == 0:
+                finish_on_tensor(0)
+            if n >= 2:
+                finish_on_vector(n - 1, 0, HALF_T)
+                finish_on_vector(n - 1, HALF_T, T)
+        finish_on_vector(NT - 1, 0, HALF_T)
+        finish_on_vector(NT - 1, HALF_T, 3 * T // 4)
+        finish_on_vector(NT - 1, 3 * T // 4, T)

@@ -31,7 +31,7 @@ X_SCALAR_RUNS = 56
 W1_VECTOR_RUNS = ((40, 80), (40, 80), (40, 80), (40, 80))
 JOINT_RUNS = 16
 W2_BEFORE_RELU = 320
-W2_VECTOR_FIRST = 192
+W2_VECTOR_FIRST = 0
 
 
 def tile_moe_res_mlp_relu_kernel(tc, xT, xr, w1, w2, gate, offs, out):
@@ -63,16 +63,19 @@ def tile_moe_res_mlp_relu_kernel(tc, xT, xr, w1, w2, gate, offs, out):
         nc.vector.memset(table[:], 0.0)
         nc.scalar.activation(out=table[:, 1:2], in_=table[:, 0:1], func=RELU)
         nc.vector.memset(gate_rows[:], 0.0)
-        nc.gpsimd.memset(x_scales[:], 0)
-        for n in range(NT):
-            nc.gpsimd.memset(windows[n][:], 0.0)
         make_identity(nc, identity[:])
+        nc.gpsimd.memset(x_scales[:].bitcast(U32), 0)
+        for n in range(NT):
+            nc.vector.memset(windows[n][:], 0.0)
 
         def rows_by_four(matrix):
             return matrix.rearrange("(p j) c -> p j c", j=J)
 
         for s in range(PASSES):
-            nc.sync.dma_start(out=x_raw[s][:], in_=rows_by_four(xT[s * K_PASS : (s + 1) * K_PASS, :]))
+            source = rows_by_four(xT[s * K_PASS : (s + 1) * K_PASS, :])
+            for half in range(2):
+                rows = slice(2 * half, 2 * half + 2)
+                nc.sync.dma_start(out=x_raw[s][:, rows, :], in_=source[:, rows, :])
             if s == 0:
                 nc.sync.dma_start(offsets[:], offs)
                 nc.sync.dma_start(out=gate_rows[0:E, :], in_=gate[0:1, :].rearrange("r (e c) -> (r e) c", e=E))
@@ -113,7 +116,7 @@ def tile_moe_res_mlp_relu_kernel(tc, xT, xr, w1, w2, gate, offs, out):
         scales_first = keep.tile([P, C], U8, name="scales_first", align_bytes=64)
         nc.vector.tensor_copy(codes_first[:], x_codes[1][:].indirect(slot_offsets(0, S)))
         nc.vector.tensor_copy(scales_first[:], x_scales[:].indirect(slot_offsets(0, C)))
-        scales_rest = first.tile([P, S - C], U8, name="scales_rest", align_bytes=64, offset=w1_bytes)
+        scales_rest = first.tile([P, S - C], U8, name="scales_rest", align_bytes=64, offset=0)
 
         def slot_operand(e, s):
             rest = slice((e - 1) * C, e * C)
@@ -243,6 +246,8 @@ def tile_moe_res_mlp_relu_kernel(tc, xT, xr, w1, w2, gate, offs, out):
             if e > 0:
                 tiles = groups[e - 1][1]
                 scatter(e - 1, tiles, sums[1], w1_raw[e][:, 1, 0 : len(tiles), 0:C])
+            else:
+                nc.vector.tensor_copy(scales_rest[:], x_scales[:].indirect(slot_offsets(C, S)))
             acc = first_layer(e, codes, scales)
             grouped = ring.tile([P, N * J], BF16, name="w2_grouped", align_bytes=64)
             codes = ring.tile([P, N], U32, name="w2_codes", align_bytes=64)
@@ -261,8 +266,6 @@ def tile_moe_res_mlp_relu_kernel(tc, xT, xr, w1, w2, gate, offs, out):
             if cut < N:
                 round_w2(nc.vector.tensor_copy, e, grouped, cut, N)
             quantise(grouped[:, HALF_N * J :], codes[:, HALF_N:], scales[:, HALF_N:])
-            if e == 0:
-                nc.vector.tensor_copy(scales_rest[:], x_scales[:].indirect(slot_offsets(C, S)))
             if e < E - 1:
                 sums = [second_layer(tiles, codes, scales, h_codes, h_scales) for tiles in groups[e]]
                 y = ring.tile([P, len(groups[e][0]), C], F32, name=f"y_first{e}")

@@ -55,7 +55,7 @@ def tile_moe_res_mlp_relu_kernel(tc, xT, xr, w1, w2, gate, offs, out):
         residual = big.tile([P, NT, T], F32, name="big")
         w1_bytes = PASSES * J * H * 4
         w1_raw = [first.tile([P, PASSES, J, H], F32, name="w1_raw0", align_bytes=64, offset=0)]
-        w1_raw.extend(keep.tile([P, PASSES, J, H], F32, name=f"w1_raw{e}") for e in range(1, E))
+        w1_raw.extend(keep.tile([P, PASSES, J, H], F32, name=f"w1_raw{e}", align_bytes=64) for e in range(1, E))
         w2_raw = [first.tile([P, J, N], F32, name="w2_raw0", align_bytes=64, offset=w1_bytes)]
         w2_raw.extend(keep.tile([P, J, N], F32, name=f"w2_raw{e}", align_bytes=64) for e in range(1, E))
 
@@ -183,9 +183,9 @@ def tile_moe_res_mlp_relu_kernel(tc, xT, xr, w1, w2, gate, offs, out):
             quantise(hidden, h_codes[:], h_scales[:])
             return h_codes, h_scales
 
-        def round_w2(copy, e, grouped, first_column, end_column):
-            copy(
-                out=grouped[:, first_column * J : end_column * J].rearrange("p (c i j) -> p c j i", i=4, j=J),
+        def round_w2(e, grouped, first_column, end_column):
+            nc.scalar.copy(
+                out=grouped.rearrange("p (c i j) -> p c j i", i=4, j=J),
                 in_=w2_raw[e][:, :, first_column:end_column].rearrange("p j (c i) -> p c j i", i=4),
             )
 
@@ -239,37 +239,38 @@ def tile_moe_res_mlp_relu_kernel(tc, xT, xr, w1, w2, gate, offs, out):
                 nc.scalar.copy(out=result[:], in_=back[:].rearrange("p b c -> p (b c)"))
                 nc.scalar.dma_start(out=out[n * P : (n + 1) * P, half * HALF_T : (half + 1) * HALF_T], in_=result[:])
 
-        groups = (((0,), (1, 2), (3,)), ((0,), (1, 2), (3,)), ((0,), (1, 2), (3,)))
-        sums = []
+        def last_tile_codes(e, grouped, codes, scales):
+            round_w2(e, grouped, N - P, N)
+            quantise(grouped, codes[:, N - P :], scales[:, N - P :])
+
         for e in range(E):
-            codes, scales = quantise_w1(e)
-            if e > 0:
-                tiles = groups[e - 1][1]
-                scatter(e - 1, tiles, sums[1], w1_raw[e][:, 1, 0 : len(tiles), 0:C])
-            else:
+            w1_codes, w1_scales = quantise_w1(e)
+            if e == 0:
                 nc.vector.tensor_copy(scales_rest[:], x_scales[:].indirect(slot_offsets(C, S)))
-            acc = first_layer(e, codes, scales)
+            else:
+                last_tile_codes(e - 1, w1_raw[e][:, 1, 2, 0 : 2 * P].bitcast(BF16), codes, scales)
+                scatter(e - 1, (1, 2), middle_sums, w1_raw[e][:, 1, 0:2, 0:C])
+            acc = first_layer(e, w1_codes, w1_scales)
+            if e > 0:
+                last_sums = second_layer((3,), codes, scales, h_codes, h_scales)
             grouped = ring.tile([P, N * J], BF16, name="w2_grouped", align_bytes=64)
             codes = ring.tile([P, N], U32, name="w2_codes", align_bytes=64)
             scales = ring.tile([P, N], U8, name="w2_scales", align_bytes=64)
-            round_w2(nc.scalar.copy, e, grouped, 0, HALF_N)
+            round_w2(e, grouped[:, : HALF_N * J], 0, HALF_N)
             quantise(grouped[:, : HALF_N * J], codes[:, :HALF_N], scales[:, :HALF_N])
-            before = W2_BEFORE_RELU
-            if before > HALF_N:
-                round_w2(nc.scalar.copy, e, grouped, HALF_N, before)
+            round_w2(e, grouped[:, HALF_N * J : W2_BEFORE_RELU * J], HALF_N, W2_BEFORE_RELU)
             h_codes, h_scales = quantise_hidden(e, acc)
-            if e > 0 and len(groups[e - 1]) > 2:
-                scatter(e - 1, groups[e - 1][2], sums[2], w2_raw[e][:, 1:2, 0:C])
-            cut = N - (W2_VECTOR_FIRST if e == 0 else 0)
-            if cut > before:
-                round_w2(nc.scalar.copy, e, grouped, before, cut)
-            if cut < N:
-                round_w2(nc.vector.tensor_copy, e, grouped, cut, N)
-            quantise(grouped[:, HALF_N * J :], codes[:, HALF_N:], scales[:, HALF_N:])
+            if e > 0:
+                scatter(e - 1, (3,), last_sums, w2_raw[e][:, 1:2, 0:C])
+            if W2_BEFORE_RELU < N - P:
+                round_w2(e, grouped[:, W2_BEFORE_RELU * J : (N - P) * J], W2_BEFORE_RELU, N - P)
+            quantise(grouped[:, HALF_N * J : (N - P) * J], codes[:, HALF_N : N - P], scales[:, HALF_N : N - P])
             if e < E - 1:
-                sums = [second_layer(tiles, codes, scales, h_codes, h_scales) for tiles in groups[e]]
-                y = ring.tile([P, len(groups[e][0]), C], F32, name=f"y_first{e}")
-                scatter(e, groups[e][0], sums[0], y[:])
+                first_sums = second_layer((0,), codes, scales, h_codes, h_scales)
+                middle_sums = second_layer((1, 2), codes, scales, h_codes, h_scales)
+                y = ring.tile([P, 1, C], F32, name="y_first")
+                scatter(e, (0,), first_sums, y[:])
+        last_tile_codes(E - 1, grouped[:, (N - P) * J :], codes, scales)
         for n in range(NT):
             acc = second_layer((n,), codes, scales, h_codes, h_scales)
             y = ring.tile([P, 1, C], F32, name=f"y_last{n}")

@@ -28,7 +28,7 @@ RUNS = H // 4
 SLOT_RUNS = C // 4
 
 X_SCALAR_RUNS = 56
-W1_VECTOR_RUNS = ((40, 80), (40, 80), (40, 80), (40, 80))
+W1_VECTOR_RUNS = ((40, 80), (28, 80), (28, 80), (28, 80))
 JOINT_RUNS = 16
 W2_BEFORE_RELU = 320
 W2_VECTOR_FIRST = 0
@@ -56,8 +56,12 @@ def tile_moe_res_mlp_relu_kernel(tc, xT, xr, w1, w2, gate, offs, out):
         w1_bytes = PASSES * J * H * 4
         w1_raw = [first.tile([P, PASSES, J, H], F32, name="w1_raw0", align_bytes=64, offset=0)]
         w1_raw.extend(keep.tile([P, PASSES, J, H], F32, name=f"w1_raw{e}", align_bytes=64) for e in range(1, E))
-        w2_raw = [first.tile([P, J, N], F32, name="w2_raw0", align_bytes=64, offset=w1_bytes)]
-        w2_raw.extend(keep.tile([P, J, N], F32, name=f"w2_raw{e}", align_bytes=64) for e in range(1, E))
+        w2_raw = [first.tile([P, J, N], F32, name="w2_raw0", align_bytes=64, offset=w1_bytes)[:]]
+        w2_raw.extend(keep.tile([P, J, N], F32, name=f"w2_raw{e}", align_bytes=64)[:] for e in range(1, E - 2))
+        w2_raw.append(keep.tile([P, J, HALF_N], F32, name="w2_raw2", align_bytes=64)[:])
+        w2_last = keep.tile([P, P + J * HALF_N], F32, name="w2_last", align_bytes=64)
+        w2_raw.append(w2_last[:, P:].rearrange("p (j c) -> p j c", j=J))
+        w2_late = {e: keep.tile([P, J, HALF_N], F32, name=f"w2_late{e}", align_bytes=64)[:] for e in (E - 2, E - 1)}
 
         table = keep.tile([P, 2], F32, name="table")
         nc.vector.memset(table[:], 0.0)
@@ -73,23 +77,27 @@ def tile_moe_res_mlp_relu_kernel(tc, xT, xr, w1, w2, gate, offs, out):
 
         for s in range(PASSES):
             source = rows_by_four(xT[s * K_PASS : (s + 1) * K_PASS, :])
-            for half in range(2):
-                rows = slice(2 * half, 2 * half + 2)
-                nc.sync.dma_start(out=x_raw[s][:, rows, :], in_=source[:, rows, :])
+            nc.sync.dma_start(out=x_raw[s][:], in_=source)
             if s == 0:
                 nc.sync.dma_start(offsets[:], offs)
                 nc.sync.dma_start(out=gate_rows[0:E, :], in_=gate[0:1, :].rearrange("r (e c) -> (r e) c", e=E))
         for e in range(E):
             for s in range(PASSES):
                 nc.sync.dma_start(out=w1_raw[e][:, s], in_=rows_by_four(w1[e][s * K_PASS : (s + 1) * K_PASS, :]))
-            nc.sync.dma_start(out=w2_raw[e][:], in_=rows_by_four(w2[e]))
+            if e < E - 2:
+                nc.sync.dma_start(out=w2_raw[e], in_=rows_by_four(w2[e]))
+            if e == E - 2:
+                nc.sync.dma_start(out=w2_raw[e], in_=rows_by_four(w2[e])[:, :, :HALF_N])
+        nc.sync.dma_start(out=w2_late[E - 2], in_=rows_by_four(w2[E - 2])[:, :, HALF_N:])
+        nc.sync.dma_start(out=w2_raw[E - 1], in_=rows_by_four(w2[E - 1])[:, :, :HALF_N])
+        nc.sync.dma_start(out=w2_late[E - 1], in_=rows_by_four(w2[E - 1])[:, :, HALF_N:])
         for n in range(NT):
             nc.sync.dma_start(out=residual[:, n, :], in_=xr[n * P : (n + 1) * P, :])
 
-        turned_gate = psum.tile([P, P], F32, name="turned_sums0")
+        turned_gate = psum.tile([P, P], F32, name="bank6")
         nc.tensor.transpose(turned_gate[:], gate_rows[:], identity[:])
         nc.scalar.copy(out=gate_columns[:], in_=turned_gate[:, 0:E])
-        spread_gate = psum.tile([P, E, C], F32, name="turned_sums1")
+        spread_gate = psum.tile([P, E, C], F32, name="bank5")
         for e in range(E):
             nc.tensor.transpose(spread_gate[:, e, :], gate_columns[:, e : e + 1].to_broadcast([P, P]), identity[:])
         nc.scalar.copy(out=gates[:], in_=spread_gate[:])
@@ -138,12 +146,10 @@ def tile_moe_res_mlp_relu_kernel(tc, xT, xr, w1, w2, gate, offs, out):
             cuts = [RUNS - runs for runs in W1_VECTOR_RUNS[e]]
             rounded(nc.scalar.copy, 0, JOINT_RUNS, JOINT_RUNS + SLOT_RUNS)
             rounded(nc.scalar.copy, 0, JOINT_RUNS + SLOT_RUNS, cuts[0])
-            if cuts[0] < RUNS:
-                rounded(nc.vector.tensor_copy, 0, cuts[0], RUNS)
+            rounded(nc.vector.tensor_copy, 0, cuts[0], RUNS)
             rounded(nc.scalar.copy, slice(0, PASSES), 0, JOINT_RUNS)
             rounded(nc.scalar.copy, 1, JOINT_RUNS, SLOT_RUNS)
-            if cuts[1] > SLOT_RUNS:
-                rounded(nc.scalar.copy, 1, SLOT_RUNS, cuts[1])
+            rounded(nc.scalar.copy, 1, SLOT_RUNS, cuts[1])
             rounded(nc.vector.tensor_copy, 1, cuts[1], RUNS)
             codes = ring.tile([P, PASSES, H], U32, name="w1_codes", align_bytes=64)
             scales = ring.tile([P, PASSES, H], U8, name="w1_scales", align_bytes=64)
@@ -155,7 +161,7 @@ def tile_moe_res_mlp_relu_kernel(tc, xT, xr, w1, w2, gate, offs, out):
             return codes, scales
 
         def first_layer(e, codes, scales):
-            acc = psum.tile([P, J, C], F32, name=f"hidden_sums{e % 2}")
+            acc = psum.tile([P, J, C], F32, name=f"bank{e % 2}")
             for t in range(J):
                 channels = slice(t * P, (t + 1) * P)
                 for s in range(PASSES):
@@ -171,8 +177,7 @@ def tile_moe_res_mlp_relu_kernel(tc, xT, xr, w1, w2, gate, offs, out):
                     )
             return acc
 
-        def quantise_hidden(e, acc):
-            hidden = w2_raw[e][:, 0, 0:HALF_N].bitcast(BF16)
+        def quantise_hidden(acc, hidden):
             nc.scalar.activation(
                 out=hidden.rearrange("p (c t) -> p c t", t=J),
                 in_=acc[:].rearrange("p t c -> p c t"),
@@ -184,13 +189,17 @@ def tile_moe_res_mlp_relu_kernel(tc, xT, xr, w1, w2, gate, offs, out):
             return h_codes, h_scales
 
         def round_w2(e, grouped, first_column, end_column):
+            if e in w2_late and first_column >= HALF_N:
+                source = w2_late[e][:, :, first_column - HALF_N : end_column - HALF_N]
+            else:
+                source = w2_raw[e][:, :, first_column:end_column]
             nc.scalar.copy(
                 out=grouped.rearrange("p (c i j) -> p c j i", i=4, j=J),
-                in_=w2_raw[e][:, :, first_column:end_column].rearrange("p j (c i) -> p c j i", i=4),
+                in_=source.rearrange("p j (c i) -> p c j i", i=4),
             )
 
-        def second_layer(tiles, codes, scales, h_codes, h_scales):
-            acc = psum.tile([P, len(tiles), C], F32, name=f"result_sums{tiles[0]}")
+        def second_layer(bank, tiles, codes, scales, h_codes, h_scales):
+            acc = psum.tile([P, len(tiles), C], F32, name=f"bank{bank}")
             for i, n in enumerate(tiles):
                 nc.tensor.matmul_mx(
                     out=acc[:, i, :],
@@ -203,83 +212,128 @@ def tile_moe_res_mlp_relu_kernel(tc, xT, xr, w1, w2, gate, offs, out):
                 )
             return acc
 
+        def scatter_tile(e, n, y):
+            nc.vector.tensor_tensor(windows[n][:].indirect(slot_offsets(e * C, (e + 1) * C)), y, gates[:, e, :], MULT)
+
         def scatter(e, tiles, acc, y):
             nc.scalar.copy(out=y, in_=acc[:])
             for i, n in enumerate(tiles):
-                nc.vector.tensor_tensor(
-                    windows[n][:].indirect(slot_offsets(e * C, (e + 1) * C)), y[:, i, :], gates[:, e, :], MULT
-                )
+                scatter_tile(e, n, y[:, i, :])
 
         def finish_on_vector(n, first_token, end_token):
             tokens = slice(first_token, end_token)
             nc.vector.tensor_tensor(residual[:, n, tokens], windows[n][:, tokens], residual[:, n, tokens], ADD)
             nc.sync.dma_start(out=out[n * P : (n + 1) * P, tokens], in_=residual[:, n, tokens])
 
-        def finish_on_tensor(n):
-            banks = [psum.tile([P, J, P], F32, name=f"turned_sums{half}") for half in range(2)]
+        def turn_on_tensor(n):
+            banks = [psum.tile([P, 2, P], F32, name=f"bank{4 + quarter}") for quarter in range(4)]
             for source, opens in ((residual[:, n], True), (windows[n][:], False)):
-                for half in range(2):
-                    for b in range(J):
-                        first_token = half * HALF_T + b * P
+                for quarter in range(4):
+                    for b in range(2):
+                        first_token = (2 * quarter + b) * P
                         nc.tensor.matmul(
-                            banks[half][:, b, :],
+                            banks[quarter][:, b, :],
                             source[:, first_token : first_token + P],
                             identity[:],
                             is_transpose=True,
                             start=(opens and b == 0),
-                            stop=(not opens and b == J - 1),
+                            stop=(not opens and b == 1),
                         )
+            turned = [ring.tile([P, 2, P], F32, name=f"turned{quarter % 2}") for quarter in range(4)]
+            for quarter in range(4):
+                nc.scalar.copy(out=turned[quarter][:], in_=banks[quarter][:])
+            return turned
+
+        def finish_on_tensor(n, turned):
             for half in range(2):
-                turned = ring.tile([P, J, P], F32, name="turned")
-                nc.scalar.copy(out=turned[:], in_=banks[half][:])
-                back = psum.tile([P, J, P], F32, name=f"hidden_sums{half}")
+                back = psum.tile([P, J, P], F32, name=f"bank{half}")
                 for b in range(J):
-                    nc.tensor.transpose(back[:, b, :], turned[:, b, :], identity[:])
+                    nc.tensor.transpose(back[:, b, :], turned[2 * half + b // 2][:, b % 2, :], identity[:])
                 result = ring.tile([P, HALF_T], F32, name="result")
                 nc.scalar.copy(out=result[:], in_=back[:].rearrange("p b c -> p (b c)"))
                 nc.scalar.dma_start(out=out[n * P : (n + 1) * P, half * HALF_T : (half + 1) * HALF_T], in_=result[:])
 
-        def last_tile_codes(e, grouped, codes, scales):
-            round_w2(e, grouped, N - P, N)
-            quantise(grouped, codes[:, N - P :], scales[:, N - P :])
+        def w2_tiles():
+            codes = ring.tile([P, N], U32, name="w2_codes", align_bytes=64)
+            scales = ring.tile([P, N], U8, name="w2_scales", align_bytes=64)
+            return codes, scales
 
-        for e in range(E):
+        def quantise_w2(e, grouped, first_column, end_column):
+            round_w2(e, grouped, first_column, end_column)
+            quantise(grouped, w2_mx[e][0][:, first_column:end_column], w2_mx[e][1][:, first_column:end_column])
+
+        def fresh(shape, dtype, name):
+            return ring.tile(shape, dtype, name=name, align_bytes=64)[:]
+
+        def products(bank, e, tiles):
+            return second_layer(bank, tiles, *w2_mx[e], *hidden_mx[e])
+
+        hidden_mx = []
+        w2_mx = []
+        last = E - 1
+        for e in range(last):
             w1_codes, w1_scales = quantise_w1(e)
             if e == 0:
                 nc.vector.tensor_copy(scales_rest[:], x_scales[:].indirect(slot_offsets(C, S)))
             else:
-                last_tile_codes(e - 1, w1_raw[e][:, 1, 2, 0 : 2 * P].bitcast(BF16), codes, scales)
+                quantise_w2(e - 1, w1_raw[e][:, 0, 1, 0 : 2 * P].bitcast(BF16), N - P, N)
                 scatter(e - 1, (1, 2), middle_sums, w1_raw[e][:, 1, 0:2, 0:C])
             acc = first_layer(e, w1_codes, w1_scales)
             if e > 0:
-                last_sums = second_layer((3,), codes, scales, h_codes, h_scales)
-            grouped = ring.tile([P, N * J], BF16, name="w2_grouped", align_bytes=64)
-            codes = ring.tile([P, N], U32, name="w2_codes", align_bytes=64)
-            scales = ring.tile([P, N], U8, name="w2_scales", align_bytes=64)
-            round_w2(e, grouped[:, : HALF_N * J], 0, HALF_N)
-            quantise(grouped[:, : HALF_N * J], codes[:, :HALF_N], scales[:, :HALF_N])
-            round_w2(e, grouped[:, HALF_N * J : W2_BEFORE_RELU * J], HALF_N, W2_BEFORE_RELU)
-            h_codes, h_scales = quantise_hidden(e, acc)
+                last_sums = products(7, e - 1, (3,))
+            grouped = fresh([P, N * J], BF16, "w2_grouped")
+            w2_mx.append(w2_tiles())
+            quantise_w2(e, grouped[:, : HALF_N * J], 0, HALF_N)
+            if e < last - 1:
+                round_w2(e, grouped[:, HALF_N * J : W2_BEFORE_RELU * J], HALF_N, W2_BEFORE_RELU)
+                hidden_mx.append(quantise_hidden(acc, w2_raw[e][:, 0, 0:HALF_N].bitcast(BF16)))
+            else:
+                hidden_mx.append(quantise_hidden(acc, fresh([P, C * J], BF16, "hidden")))
             if e > 0:
                 scatter(e - 1, (3,), last_sums, w2_raw[e][:, 1:2, 0:C])
-            if W2_BEFORE_RELU < N - P:
+            if e < last - 1:
                 round_w2(e, grouped[:, W2_BEFORE_RELU * J : (N - P) * J], W2_BEFORE_RELU, N - P)
-            quantise(grouped[:, HALF_N * J : (N - P) * J], codes[:, HALF_N : N - P], scales[:, HALF_N : N - P])
-            if e < E - 1:
-                first_sums = second_layer((0,), codes, scales, h_codes, h_scales)
-                middle_sums = second_layer((1, 2), codes, scales, h_codes, h_scales)
-                y = ring.tile([P, 1, C], F32, name="y_first")
-                scatter(e, (0,), first_sums, y[:])
-        last_tile_codes(E - 1, grouped[:, (N - P) * J :], codes, scales)
-        for n in range(NT):
-            acc = second_layer((n,), codes, scales, h_codes, h_scales)
-            y = ring.tile([P, 1, C], F32, name=f"y_last{n}")
-            scatter(E - 1, (n,), acc, y[:])
-            if n == 0:
-                finish_on_tensor(0)
-            if n >= 2:
-                finish_on_vector(n - 1, 0, HALF_T)
-                finish_on_vector(n - 1, HALF_T, T)
-        finish_on_vector(NT - 1, 0, HALF_T)
-        finish_on_vector(NT - 1, HALF_T, 3 * T // 4)
-        finish_on_vector(NT - 1, 3 * T // 4, T)
+                quantise(
+                    grouped[:, HALF_N * J : (N - P) * J],
+                    w2_mx[e][0][:, HALF_N : N - P],
+                    w2_mx[e][1][:, HALF_N : N - P],
+                )
+                first_sums = products(2, e, (0,))
+                middle_sums = products(3, e, (1, 2))
+                scatter(e, (0,), first_sums, fresh([P, 1, C], F32, "y_first"))
+            else:
+                first_sums = products(2, e, (0,))
+                middle_sums = products(3, e, (1,))
+
+        w1_codes, w1_scales = quantise_w1(last)
+        scatter(last - 1, (0,), first_sums, w1_raw[last][:, 1, 0:1, 0:C])
+        quantise_w2(last - 1, grouped[:, HALF_N * J : (N - P) * J], HALF_N, N - P)
+        scatter(last - 1, (1,), middle_sums, w2_late[last - 1][:, 0:1, 0:C])
+        acc = first_layer(last, w1_codes, w1_scales)
+        third_sums = products(2, last - 1, (2,))
+        grouped = fresh([P, N * J], BF16, "w2_grouped")
+        w2_mx.append(w2_tiles())
+        round_w2(last, grouped[:, : P * J], 0, P)
+        round_w2(last, grouped[:, P * J : HALF_N * J], P, HALF_N)
+        quantise(grouped[:, : HALF_N * J], w2_mx[last][0][:, :HALF_N], w2_mx[last][1][:, :HALF_N])
+        hidden_mx.append(quantise_hidden(acc, w2_last[:, : 2 * P].bitcast(BF16)))
+        scatter(last - 1, (2,), third_sums, w2_raw[last][:, 1:2, 0:C])
+        scatter(last, (0,), products(3, last, (0,)), fresh([P, 1, C], F32, "y_last0"))
+        scatter(last, (1,), products(2, last, (1,)), fresh([P, 1, C], F32, "y_last1"))
+        for n in (2, 3):
+            quantise_w2(last, grouped[:, n * P * J : (n + 1) * P * J], n * P, (n + 1) * P)
+        quantise_w2(last - 1, w2_raw[last][:, 2, 0:HALF_N].bitcast(BF16), N - P, N)
+        finish_on_vector(1, 0, HALF_T)
+        finish_on_vector(1, HALF_T, T)
+        scatter(last, (2,), products(3, last, (2,)), fresh([P, 1, C], F32, "y_last2"))
+        scatter(last, (3,), products(2, last, (3,)), fresh([P, 1, C], F32, "y_last3"))
+        turned = turn_on_tensor(0)
+        held = fresh([P, 1, C], F32, "y_last0")
+        nc.scalar.copy(out=held, in_=products(3, last - 1, (3,))[:])
+        finish_on_tensor(0, turned)
+        finish_on_vector(2, 0, HALF_T)
+        scatter_tile(last - 1, 3, held[:, 0, :])
+        finish_on_vector(2, HALF_T, T)
+        finish_on_vector(3, 0, HALF_T)
+        finish_on_vector(3, HALF_T, 3 * T // 4)
+        finish_on_vector(3, 3 * T // 4, T)

@@ -220,9 +220,9 @@ def tile_moe_res_mlp_relu_kernel(tc, xT, xr, w1, w2, gate, offs, out):
             for i, n in enumerate(tiles):
                 scatter_tile(e, n, y[:, i, :])
 
-        def finish_on_vector(n, first_token, end_token):
+        def finish_on_vector(n, first_token, end_token, engine=nc.vector):
             tokens = slice(first_token, end_token)
-            nc.vector.tensor_tensor(residual[:, n, tokens], windows[n][:, tokens], residual[:, n, tokens], ADD)
+            engine.tensor_tensor(residual[:, n, tokens], windows[n][:, tokens], residual[:, n, tokens], ADD)
             nc.sync.dma_start(out=out[n * P : (n + 1) * P, tokens], in_=residual[:, n, tokens])
 
         def turn_on_tensor(n):
@@ -246,7 +246,7 @@ def tile_moe_res_mlp_relu_kernel(tc, xT, xr, w1, w2, gate, offs, out):
 
         def finish_on_tensor(n, turned):
             for half in range(2):
-                back = psum.tile([P, J, P], F32, name=f"bank{half}")
+                back = psum.tile([P, J, P], F32, name=f"bank{1 + half}")
                 for b in range(J):
                     nc.tensor.transpose(back[:, b, :], turned[2 * half + b // 2][:, b % 2, :], identity[:])
                 result = ring.tile([P, HALF_T], F32, name="result")
@@ -319,20 +319,23 @@ def tile_moe_res_mlp_relu_kernel(tc, xT, xr, w1, w2, gate, offs, out):
         hidden_mx.append(quantise_hidden(acc, w2_last[:, : 2 * P].bitcast(BF16)))
         scatter(last - 1, (2,), third_sums, w2_raw[last][:, 1:2, 0:C])
         scatter(last, (0,), products(3, last, (0,)), fresh([P, 1, C], F32, "y_last0"))
-        scatter(last, (1,), products(2, last, (1,)), fresh([P, 1, C], F32, "y_last1"))
+        second_sums = products(2, last, (1,))
         for n in (2, 3):
             quantise_w2(last, grouped[:, n * P * J : (n + 1) * P * J], n * P, (n + 1) * P)
         quantise_w2(last - 1, w2_raw[last][:, 2, 0:HALF_N].bitcast(BF16), N - P, N)
-        finish_on_vector(1, 0, HALF_T)
-        finish_on_vector(1, HALF_T, T)
-        scatter(last, (2,), products(3, last, (2,)), fresh([P, 1, C], F32, "y_last2"))
-        scatter(last, (3,), products(2, last, (3,)), fresh([P, 1, C], F32, "y_last3"))
-        turned = turn_on_tensor(0)
-        held = fresh([P, 1, C], F32, "y_last0")
-        nc.scalar.copy(out=held, in_=products(3, last - 1, (3,))[:])
-        finish_on_tensor(0, turned)
+        gated = fresh([P, 2, C], F32, "gated")
+        last_gates = gates[:, last : last + 1, :].to_broadcast([P, 2, C])
+        nc.vector.tensor_tensor(gated, products(3, last, (2, 3))[:], last_gates, MULT)
+        scatter(last, (1,), second_sums, w2_late[last - 1][:, 1:2, C:])
+        held = fresh([P, C], F32, "gated_held")
+        nc.vector.tensor_tensor(held, products(0, last - 1, (3,))[:, 0, :], gates[:, last - 1, :], MULT)
+        finish_on_vector(1, 0, HALF_T, nc.gpsimd)
+        finish_on_vector(1, HALF_T, T, nc.gpsimd)
+        for i in (1, 0):
+            nc.vector.tensor_copy(windows[2 + i][:].indirect(slot_offsets(last * C, S)), gated[:, i, :])
+        nc.vector.tensor_copy(windows[3][:].indirect(slot_offsets((last - 1) * C, last * C)), held)
+        finish_on_tensor(0, turn_on_tensor(0))
         finish_on_vector(2, 0, HALF_T)
-        scatter_tile(last - 1, 3, held[:, 0, :])
         finish_on_vector(2, HALF_T, T)
         finish_on_vector(3, 0, HALF_T)
         finish_on_vector(3, HALF_T, 3 * T // 4)

@@ -38,7 +38,7 @@ def tile_moe_res_mlp_relu_kernel(tc, xT, xr, w1, w2, gate, offs, out):
     nc = tc.nc
     with ExitStack() as ctx:
         keep = ctx.enter_context(tc.tile_pool(name="keep", bufs=1))
-        big = ctx.enter_context(tc.tile_pool(name="big", bufs=2))
+        big = ctx.enter_context(tc.tile_pool(name="big", bufs=1))
         ring = ctx.enter_context(tc.tile_pool(name="ring", bufs=2))
         first = ctx.enter_context(tc.tile_pool(name="first", bufs=1))
         psum = ctx.enter_context(tc.psum_pool(name="psum", bufs=1))
@@ -51,8 +51,10 @@ def tile_moe_res_mlp_relu_kernel(tc, xT, xr, w1, w2, gate, offs, out):
         x_codes = [keep.tile([P, T], U32, name=f"x_codes{s}", align_bytes=64) for s in range(PASSES)]
         x_scales = keep.tile([P, T], U8, name="x_scales", align_bytes=64)
         windows = [keep.tile([P, T], F32, name=f"window{n}") for n in range(NT)]
-        x_raw = [big.tile([P, J, T], F32, name="big") for s in range(PASSES)]
-        residual = big.tile([P, NT, T], F32, name="big")
+        x_raw = [big.tile([P, J, T], F32, name=f"x_raw{s}", offset=s * J * T * 4) for s in range(PASSES)]
+        second_halves = big.tile([P, 2, HALF_T], F32, name="second_halves", offset=0)
+        first_halves = big.tile([P, 2, HALF_T], F32, name="first_halves", offset=T * 4)
+        residual = {n: big.tile([P, T], F32, name=f"residual{n}", offset=n * T * 4)[:] for n in (2, 3)}
         w1_bytes = PASSES * J * H * 4
         w1_raw = [first.tile([P, PASSES, J, H], F32, name="w1_raw0", align_bytes=64, offset=0)]
         w1_raw.extend(keep.tile([P, PASSES, J, H], F32, name=f"w1_raw{e}", align_bytes=64) for e in range(1, E))
@@ -91,8 +93,11 @@ def tile_moe_res_mlp_relu_kernel(tc, xT, xr, w1, w2, gate, offs, out):
         nc.sync.dma_start(out=w2_late[E - 2], in_=rows_by_four(w2[E - 2])[:, :, HALF_N:])
         nc.sync.dma_start(out=w2_raw[E - 1], in_=rows_by_four(w2[E - 1])[:, :, :HALF_N])
         nc.sync.dma_start(out=w2_late[E - 1], in_=rows_by_four(w2[E - 1])[:, :, HALF_N:])
-        for n in range(NT):
-            nc.sync.dma_start(out=residual[:, n, :], in_=xr[n * P : (n + 1) * P, :])
+        two_tiles = xr[: 2 * P, :].rearrange("(n p) t -> p n t", p=P)
+        nc.sync.dma_start(out=second_halves[:], in_=two_tiles[:, :, HALF_T:])
+        nc.sync.dma_start(out=first_halves[:], in_=two_tiles[:, :, :HALF_T])
+        for n in (2, 3):
+            nc.sync.dma_start(out=residual[n], in_=xr[n * P : (n + 1) * P, :])
 
         turned_gate = psum.tile([P, P], F32, name="bank6")
         nc.tensor.transpose(turned_gate[:], gate_rows[:], identity[:])
@@ -153,18 +158,18 @@ def tile_moe_res_mlp_relu_kernel(tc, xT, xr, w1, w2, gate, offs, out):
             rounded(nc.vector.tensor_copy, 1, cuts[1], RUNS)
             codes = ring.tile([P, PASSES, H], U32, name="w1_codes", align_bytes=64)
             scales = ring.tile([P, PASSES, H], U8, name="w1_scales", align_bytes=64)
+            quantise(grouped[:, 0], codes[:, 0], scales[:, 0])
             for half in range(2):
-                for s in range(PASSES):
-                    columns = slice(half * H // 2, (half + 1) * H // 2)
-                    values = slice(half * H * J // 2, (half + 1) * H * J // 2)
-                    quantise(grouped[:, s, values], codes[:, s, columns], scales[:, s, columns])
+                columns = slice(half * H // 2, (half + 1) * H // 2)
+                values = slice(half * H * J // 2, (half + 1) * H * J // 2)
+                quantise(grouped[:, 1, values], codes[:, 1, columns], scales[:, 1, columns])
             return codes, scales
 
         def first_layer(e, codes, scales):
             acc = psum.tile([P, J, C], F32, name=f"bank{e % 2}")
-            for t in range(J):
-                channels = slice(t * P, (t + 1) * P)
-                for s in range(PASSES):
+            for s in range(PASSES):
+                for t in range(J):
+                    channels = slice(t * P, (t + 1) * P)
                     x_words, x_bytes = slot_operand(e, s)
                     nc.tensor.matmul_mx(
                         out=acc[:, t, :],
@@ -172,8 +177,8 @@ def tile_moe_res_mlp_relu_kernel(tc, xT, xr, w1, w2, gate, offs, out):
                         lhsT_scale=scales[:, s, channels],
                         rhs=x_words.bitcast(FP8X4),
                         rhs_scale=x_bytes,
-                        start=(s == 0),
-                        stop=(s == PASSES - 1),
+                        start=(s == 0 and t == 0),
+                        stop=(s == PASSES - 1 and t == J - 1),
                     )
             return acc
 
@@ -220,38 +225,36 @@ def tile_moe_res_mlp_relu_kernel(tc, xT, xr, w1, w2, gate, offs, out):
             for i, n in enumerate(tiles):
                 scatter_tile(e, n, y[:, i, :])
 
-        def finish_on_vector(n, first_token, end_token, engine=nc.vector):
+        def finish(engine, n, first_token, end_token, total):
             tokens = slice(first_token, end_token)
-            engine.tensor_tensor(residual[:, n, tokens], windows[n][:, tokens], residual[:, n, tokens], ADD)
-            nc.sync.dma_start(out=out[n * P : (n + 1) * P, tokens], in_=residual[:, n, tokens])
+            addend = first_halves[:, n] if n < 2 else residual[n][:, tokens]
+            engine.tensor_tensor(total, windows[n][:, tokens], addend, ADD)
+            nc.sync.dma_start(out=out[n * P : (n + 1) * P, tokens], in_=total)
 
-        def turn_on_tensor(n):
-            banks = [psum.tile([P, 2, P], F32, name=f"bank{4 + quarter}") for quarter in range(4)]
-            for source, opens in ((residual[:, n], True), (windows[n][:], False)):
-                for quarter in range(4):
-                    for b in range(2):
-                        first_token = (2 * quarter + b) * P
-                        nc.tensor.matmul(
-                            banks[quarter][:, b, :],
-                            source[:, first_token : first_token + P],
-                            identity[:],
-                            is_transpose=True,
-                            start=(opens and b == 0),
-                            stop=(not opens and b == 1),
-                        )
-            turned = [ring.tile([P, 2, P], F32, name=f"turned{quarter % 2}") for quarter in range(4)]
-            for quarter in range(4):
-                nc.scalar.copy(out=turned[quarter][:], in_=banks[quarter][:])
-            return turned
+        def turn(source, banks, opens):
+            for block in range(4):
+                nc.tensor.matmul(
+                    banks[block // 2][:, block % 2, :],
+                    source[:, block * P : (block + 1) * P],
+                    identity[:],
+                    is_transpose=True,
+                    start=(opens and block % 2 == 0),
+                    stop=(not opens and block % 2 == 1),
+                )
 
-        def finish_on_tensor(n, turned):
-            for half in range(2):
-                back = psum.tile([P, J, P], F32, name=f"bank{1 + half}")
-                for b in range(J):
-                    nc.tensor.transpose(back[:, b, :], turned[2 * half + b // 2][:, b % 2, :], identity[:])
-                result = ring.tile([P, HALF_T], F32, name="result")
-                nc.scalar.copy(out=result[:], in_=back[:].rearrange("p b c -> p (b c)"))
-                nc.scalar.dma_start(out=out[n * P : (n + 1) * P, half * HALF_T : (half + 1) * HALF_T], in_=result[:])
+        def finish_on_tensor(n):
+            banks = [psum.tile([P, 2, P], F32, name=f"bank{4 + 2 * n + pair}") for pair in range(2)]
+            turn(second_halves[:, n], banks, True)
+            turn(windows[n][:, HALF_T:], banks, False)
+            turned = [ring.tile([P, 2, P], F32, name=f"turned{pair}") for pair in range(2)]
+            for pair in range(2):
+                nc.scalar.copy(out=turned[pair][:], in_=banks[pair][:])
+            back = psum.tile([P, J, P], F32, name=f"bank{1 + n}")
+            for b in range(J):
+                nc.tensor.transpose(back[:, b, :], turned[b // 2][:, b % 2, :], identity[:])
+            result = ring.tile([P, HALF_T], F32, name="result")
+            nc.scalar.copy(out=result[:], in_=back[:].rearrange("p b c -> p (b c)"))
+            nc.scalar.dma_start(out=out[n * P : (n + 1) * P, HALF_T:], in_=result[:])
 
         def w2_tiles():
             codes = ring.tile([P, N], U32, name="w2_codes", align_bytes=64)
@@ -322,21 +325,34 @@ def tile_moe_res_mlp_relu_kernel(tc, xT, xr, w1, w2, gate, offs, out):
         second_sums = products(2, last, (1,))
         for n in (2, 3):
             quantise_w2(last, grouped[:, n * P * J : (n + 1) * P * J], n * P, (n + 1) * P)
-        quantise_w2(last - 1, w2_raw[last][:, 2, 0:HALF_N].bitcast(BF16), N - P, N)
-        gated = fresh([P, 2, C], F32, "gated")
-        last_gates = gates[:, last : last + 1, :].to_broadcast([P, 2, C])
-        nc.vector.tensor_tensor(gated, products(3, last, (2, 3))[:], last_gates, MULT)
-        scatter(last, (1,), second_sums, w2_late[last - 1][:, 1:2, C:])
-        held = fresh([P, C], F32, "gated_held")
-        nc.vector.tensor_tensor(held, products(0, last - 1, (3,))[:, 0, :], gates[:, last - 1, :], MULT)
-        finish_on_vector(1, 0, HALF_T, nc.gpsimd)
-        finish_on_vector(1, HALF_T, T, nc.gpsimd)
-        for i in (1, 0):
-            nc.vector.tensor_copy(windows[2 + i][:].indirect(slot_offsets(last * C, S)), gated[:, i, :])
-        nc.vector.tensor_copy(windows[3][:].indirect(slot_offsets((last - 1) * C, last * C)), held)
-        finish_on_tensor(0, turn_on_tensor(0))
-        finish_on_vector(2, 0, HALF_T)
-        finish_on_vector(2, HALF_T, T)
-        finish_on_vector(3, 0, HALF_T)
-        finish_on_vector(3, HALF_T, 3 * T // 4)
-        finish_on_vector(3, 3 * T // 4, T)
+        held_grouped = w2_raw[last][:, 2, 0:HALF_N].bitcast(BF16)
+        round_w2(last - 1, held_grouped, N - P, N)
+        gated = w2_late[last - 1][:, 0:2, C:]
+        nc.vector.tensor_tensor(gated[:, 0, :], second_sums[:, 0, :], gates[:, last, :], MULT)
+        nc.vector.tensor_tensor(gated[:, 1, :], products(3, last, (2,))[:, 0, :], gates[:, last, :], MULT)
+        quantise(held_grouped, w2_mx[last - 1][0][:, N - P :], w2_mx[last - 1][1][:, N - P :])
+        for i in range(2):
+            nc.vector.tensor_copy(windows[1 + i][:].indirect(slot_offsets(last * C, S)), gated[:, i, :])
+        pair_sums = psum.tile([P, 2, C], F32, name="bank0")
+        for e in (last, last - 1):
+            nc.tensor.matmul_mx(
+                out=pair_sums[:, e - last + 1, :],
+                lhsT=w2_mx[e][0][:, N - P :].bitcast(FP8X4),
+                lhsT_scale=w2_mx[e][1][:, N - P :],
+                rhs=hidden_mx[e][0][:].bitcast(FP8X4),
+                rhs_scale=hidden_mx[e][1][:],
+                start=True,
+                stop=True,
+            )
+        pair = fresh([P, 2, C], F32, "pair")
+        nc.vector.tensor_tensor(pair, pair_sums[:], gates[:, last - 1 :, :], MULT)
+        finish(nc.gpsimd, 0, 0, HALF_T, w2_last[:, P + 2 * HALF_N :])
+        finish_on_tensor(0)
+        nc.vector.tensor_copy(windows[3][:].indirect(slot_offsets((last - 1) * C, S)), pair.rearrange("p e c -> p (e c)"))
+        finish(nc.gpsimd, 1, 0, HALF_T, fresh([P, HALF_T], F32, "second_sum"))
+        finish_on_tensor(1)
+        finish(nc.gpsimd, 2, 0, HALF_T, fresh([P, HALF_T], F32, "third_sum"))
+        finish(nc.vector, 2, HALF_T, T, windows[2][:, :HALF_T])
+        finish(nc.vector, 3, 0, HALF_T, residual[2][:, :HALF_T])
+        finish(nc.vector, 3, HALF_T, 3 * T // 4, residual[2][:, HALF_T : 3 * T // 4])
+        finish(nc.vector, 3, 3 * T // 4, T, residual[2][:, 3 * T // 4 :])

@@ -28,10 +28,11 @@ RUNS = H // 4
 SLOT_RUNS = C // 4
 
 X_SCALAR_RUNS = 56
-W1_VECTOR_RUNS = ((40, 80), (28, 80), (28, 80), (28, 80))
+FIRST_VECTOR_RUNS = 40
+PASS0_VECTOR_RUNS = 28
+PASS1_VECTOR_RUNS = 80
 JOINT_RUNS = 16
 W2_BEFORE_RELU = 320
-W2_VECTOR_FIRST = 0
 
 
 def tile_moe_res_mlp_relu_kernel(tc, xT, xr, w1, w2, gate, offs, out):
@@ -65,9 +66,6 @@ def tile_moe_res_mlp_relu_kernel(tc, xT, xr, w1, w2, gate, offs, out):
         w2_raw.append(w2_last[:, P:].rearrange("p (j c) -> p j c", j=J))
         w2_late = {e: keep.tile([P, J, HALF_N], F32, name=f"w2_late{e}", align_bytes=64)[:] for e in (E - 2, E - 1)}
 
-        table = keep.tile([P, 2], F32, name="table")
-        nc.vector.memset(table[:], 0.0)
-        nc.scalar.activation(out=table[:, 1:2], in_=table[:, 0:1], func=RELU)
         nc.vector.memset(gate_rows[:], 0.0)
         make_identity(nc, identity[:])
         nc.gpsimd.memset(x_scales[:].bitcast(U32), 0)
@@ -125,19 +123,15 @@ def tile_moe_res_mlp_relu_kernel(tc, xT, xr, w1, w2, gate, offs, out):
             if s == 0:
                 codes_pass0 = keep.tile([P, S], U32, name="codes_pass0", align_bytes=64)
                 nc.vector.tensor_copy(codes_pass0[:], x_codes[0][:].indirect(offsets[:]))
-        codes_first = keep.tile([P, S], U32, name="codes_first", align_bytes=64)
+        codes_pass1 = keep.tile([P, S], U32, name="codes_first", align_bytes=64)
         scales_first = keep.tile([P, C], U8, name="scales_first", align_bytes=64)
-        nc.vector.tensor_copy(codes_first[:], x_codes[1][:].indirect(slot_offsets(0, S)))
+        nc.vector.tensor_copy(codes_pass1[:], x_codes[1][:].indirect(slot_offsets(0, S)))
         nc.vector.tensor_copy(scales_first[:], x_scales[:].indirect(slot_offsets(0, C)))
         scales_rest = first.tile([P, S - C], U8, name="scales_rest", align_bytes=64, offset=0)
 
         def slot_operand(e, s):
-            rest = slice((e - 1) * C, e * C)
-            if s == 0:
-                codes = codes_pass0[:, e * C : (e + 1) * C]
-            else:
-                codes = codes_first[:, e * C : (e + 1) * C]
-            scales = scales_first[4 * s : P, :] if e == 0 else scales_rest[4 * s : P, rest]
+            codes = (codes_pass0, codes_pass1)[s][:, e * C : (e + 1) * C]
+            scales = scales_first[4 * s : P, :] if e == 0 else scales_rest[4 * s : P, (e - 1) * C : e * C]
             return codes, scales
 
         def quantise_w1(e):
@@ -148,7 +142,7 @@ def tile_moe_res_mlp_relu_kernel(tc, xT, xr, w1, w2, gate, offs, out):
             def rounded(copy, passes, first_run, end_run):
                 copy(out=target[:, passes, first_run:end_run], in_=source[:, passes, first_run:end_run])
 
-            cuts = [RUNS - runs for runs in W1_VECTOR_RUNS[e]]
+            cuts = (RUNS - (FIRST_VECTOR_RUNS if e == 0 else PASS0_VECTOR_RUNS), RUNS - PASS1_VECTOR_RUNS)
             rounded(nc.scalar.copy, 0, JOINT_RUNS, JOINT_RUNS + SLOT_RUNS)
             rounded(nc.scalar.copy, 0, JOINT_RUNS + SLOT_RUNS, cuts[0])
             rounded(nc.vector.tensor_copy, 0, cuts[0], RUNS)
@@ -217,13 +211,11 @@ def tile_moe_res_mlp_relu_kernel(tc, xT, xr, w1, w2, gate, offs, out):
                 )
             return acc
 
-        def scatter_tile(e, n, y):
-            nc.vector.tensor_tensor(windows[n][:].indirect(slot_offsets(e * C, (e + 1) * C)), y, gates[:, e, :], MULT)
-
         def scatter(e, tiles, acc, y):
             nc.scalar.copy(out=y, in_=acc[:])
             for i, n in enumerate(tiles):
-                scatter_tile(e, n, y[:, i, :])
+                window = windows[n][:].indirect(slot_offsets(e * C, (e + 1) * C))
+                nc.vector.tensor_tensor(window, y[:, i, :], gates[:, e, :], MULT)
 
         def finish(engine, n, first_token, end_token, total):
             tokens = slice(first_token, end_token)
@@ -261,9 +253,12 @@ def tile_moe_res_mlp_relu_kernel(tc, xT, xr, w1, w2, gate, offs, out):
             scales = ring.tile([P, N], U8, name="w2_scales", align_bytes=64)
             return codes, scales
 
+        def quantise_columns(e, grouped, first_column, end_column):
+            quantise(grouped, w2_mx[e][0][:, first_column:end_column], w2_mx[e][1][:, first_column:end_column])
+
         def quantise_w2(e, grouped, first_column, end_column):
             round_w2(e, grouped, first_column, end_column)
-            quantise(grouped, w2_mx[e][0][:, first_column:end_column], w2_mx[e][1][:, first_column:end_column])
+            quantise_columns(e, grouped, first_column, end_column)
 
         def fresh(shape, dtype, name):
             return ring.tile(shape, dtype, name=name, align_bytes=64)[:]
@@ -296,11 +291,7 @@ def tile_moe_res_mlp_relu_kernel(tc, xT, xr, w1, w2, gate, offs, out):
                 scatter(e - 1, (3,), last_sums, w2_raw[e][:, 1:2, 0:C])
             if e < last - 1:
                 round_w2(e, grouped[:, W2_BEFORE_RELU * J : (N - P) * J], W2_BEFORE_RELU, N - P)
-                quantise(
-                    grouped[:, HALF_N * J : (N - P) * J],
-                    w2_mx[e][0][:, HALF_N : N - P],
-                    w2_mx[e][1][:, HALF_N : N - P],
-                )
+                quantise_columns(e, grouped[:, HALF_N * J : (N - P) * J], HALF_N, N - P)
                 first_sums = products(2, e, (0,))
                 middle_sums = products(3, e, (1, 2))
                 scatter(e, (0,), first_sums, fresh([P, 1, C], F32, "y_first"))
@@ -318,7 +309,7 @@ def tile_moe_res_mlp_relu_kernel(tc, xT, xr, w1, w2, gate, offs, out):
         w2_mx.append(w2_tiles())
         round_w2(last, grouped[:, : P * J], 0, P)
         round_w2(last, grouped[:, P * J : HALF_N * J], P, HALF_N)
-        quantise(grouped[:, : HALF_N * J], w2_mx[last][0][:, :HALF_N], w2_mx[last][1][:, :HALF_N])
+        quantise_columns(last, grouped[:, : HALF_N * J], 0, HALF_N)
         hidden_mx.append(quantise_hidden(acc, w2_last[:, : 2 * P].bitcast(BF16)))
         scatter(last - 1, (2,), third_sums, w2_raw[last][:, 1:2, 0:C])
         scatter(last, (0,), products(3, last, (0,)), fresh([P, 1, C], F32, "y_last0"))
@@ -330,7 +321,7 @@ def tile_moe_res_mlp_relu_kernel(tc, xT, xr, w1, w2, gate, offs, out):
         gated = w2_late[last - 1][:, 0:2, C:]
         nc.vector.tensor_tensor(gated[:, 0, :], second_sums[:, 0, :], gates[:, last, :], MULT)
         nc.vector.tensor_tensor(gated[:, 1, :], products(3, last, (2,))[:, 0, :], gates[:, last, :], MULT)
-        quantise(held_grouped, w2_mx[last - 1][0][:, N - P :], w2_mx[last - 1][1][:, N - P :])
+        quantise_columns(last - 1, held_grouped, N - P, N)
         for i in range(2):
             nc.vector.tensor_copy(windows[1 + i][:].indirect(slot_offsets(last * C, S)), gated[:, i, :])
         pair_sums = psum.tile([P, 2, C], F32, name="bank0")

@@ -16,6 +16,7 @@ FP8X4 = mybir.dt.float8_e4m3fn_x4
 ADD = mybir.AluOpType.add
 MULT = mybir.AluOpType.mult
 RELU = mybir.ActivationFunctionType.Relu
+COPY = mybir.ActivationFunctionType.Copy
 
 P = 128
 J = 4
@@ -27,21 +28,18 @@ HALF_N = N // 2
 RUNS = H // 4
 SLOT_RUNS = C // 4
 
-X_SCALAR_RUNS = 56
-FIRST_VECTOR_RUNS = 40
-PASS0_VECTOR_RUNS = 28
-PASS1_VECTOR_RUNS = 80
-JOINT_RUNS = 16
-W2_BEFORE_RELU = 320
+X_SCALAR_RUNS = 48
+FIRST_SCALAR_RUNS = 64
+PASS0_SCALAR_RUNS = 72
 
 
 def tile_moe_res_mlp_relu_kernel(tc, xT, xr, w1, w2, gate, offs, out):
     nc = tc.nc
+    last = E - 1
     with ExitStack() as ctx:
         keep = ctx.enter_context(tc.tile_pool(name="keep", bufs=1))
         big = ctx.enter_context(tc.tile_pool(name="big", bufs=1))
         ring = ctx.enter_context(tc.tile_pool(name="ring", bufs=2))
-        first = ctx.enter_context(tc.tile_pool(name="first", bufs=1))
         psum = ctx.enter_context(tc.psum_pool(name="psum", bufs=1))
 
         offsets = keep.tile([P, S // 16], U16, name="offsets")
@@ -51,20 +49,23 @@ def tile_moe_res_mlp_relu_kernel(tc, xT, xr, w1, w2, gate, offs, out):
         identity = keep.tile([P, P], F32, name="identity")
         x_codes = [keep.tile([P, T], U32, name=f"x_codes{s}", align_bytes=64) for s in range(PASSES)]
         x_scales = keep.tile([P, T], U8, name="x_scales", align_bytes=64)
+        slot_codes = [keep.tile([P, S], U32, name=f"slot_codes{s}", align_bytes=64) for s in range(PASSES)]
+        slot_scales = keep.tile([P, S], U8, name="slot_scales", align_bytes=64)
         windows = [keep.tile([P, T], F32, name=f"window{n}") for n in range(NT)]
-        x_raw = [big.tile([P, J, T], F32, name=f"x_raw{s}", offset=s * J * T * 4) for s in range(PASSES)]
-        second_halves = big.tile([P, 2, HALF_T], F32, name="second_halves", offset=0)
-        first_halves = big.tile([P, 2, HALF_T], F32, name="first_halves", offset=T * 4)
-        residual = {n: big.tile([P, T], F32, name=f"residual{n}", offset=n * T * 4)[:] for n in (2, 3)}
-        w1_bytes = PASSES * J * H * 4
-        w1_raw = [first.tile([P, PASSES, J, H], F32, name="w1_raw0", align_bytes=64, offset=0)]
-        w1_raw.extend(keep.tile([P, PASSES, J, H], F32, name=f"w1_raw{e}", align_bytes=64) for e in range(1, E))
-        w2_raw = [first.tile([P, J, N], F32, name="w2_raw0", align_bytes=64, offset=w1_bytes)[:]]
-        w2_raw.extend(keep.tile([P, J, N], F32, name=f"w2_raw{e}", align_bytes=64)[:] for e in range(1, E - 2))
-        w2_raw.append(keep.tile([P, J, HALF_N], F32, name="w2_raw2", align_bytes=64)[:])
-        w2_last = keep.tile([P, P + J * HALF_N], F32, name="w2_last", align_bytes=64)
-        w2_raw.append(w2_last[:, P:].rearrange("p (j c) -> p j c", j=J))
-        w2_late = {e: keep.tile([P, J, HALF_N], F32, name=f"w2_late{e}", align_bytes=64)[:] for e in (E - 2, E - 1)}
+        x_first = big.tile([P, J, T], F32, name="x_first", offset=0)
+        x_halves = [big.tile([P, J, HALF_T], F32, name=f"x_half{h}", offset=(2 + h) * J * HALF_T * 4) for h in range(2)]
+        x_raw = [[x_first[:, :, :HALF_T], x_first[:, :, HALF_T:]], [x_halves[0][:], x_halves[1][:]]]
+        residual = [big.tile([P, 2, T], F32, name=f"residual{h}", offset=h * 2 * T * 4) for h in range(2)]
+        w1_raw = [
+            [keep.tile([P, J, H], F32, name=f"w1_raw{e}_{s}", align_bytes=64) for s in range(PASSES)] for e in range(E)
+        ]
+        w2_cuts = [(0, N)] * (E - 2) + [(0, N - P, N), (0, HALF_N, N)]
+        w2_raw = [
+            [keep.tile([P, J, b - a], F32, name=f"w2_raw{e}_{a}", align_bytes=64) for a, b in zip(cuts, cuts[1:])]
+            for e, cuts in enumerate(w2_cuts)
+        ]
+        w2_codes = [keep.tile([P, N], U32, name=f"w2_codes{e}", align_bytes=64) for e in range(E)]
+        w2_scales = [keep.tile([P, N], U8, name=f"w2_scales{e}", align_bytes=64) for e in range(E)]
 
         nc.vector.memset(gate_rows[:], 0.0)
         make_identity(nc, identity[:])
@@ -75,27 +76,23 @@ def tile_moe_res_mlp_relu_kernel(tc, xT, xr, w1, w2, gate, offs, out):
         def rows_by_four(matrix):
             return matrix.rearrange("(p j) c -> p j c", j=J)
 
-        for s in range(PASSES):
-            source = rows_by_four(xT[s * K_PASS : (s + 1) * K_PASS, :])
-            nc.sync.dma_start(out=x_raw[s][:], in_=source)
-            if s == 0:
-                nc.sync.dma_start(offsets[:], offs)
-                nc.sync.dma_start(out=gate_rows[0:E, :], in_=gate[0:1, :].rearrange("r (e c) -> (r e) c", e=E))
+        def load_w2(e, piece):
+            columns = slice(w2_cuts[e][piece], w2_cuts[e][piece + 1])
+            nc.sync.dma_start(out=w2_raw[e][piece][:], in_=rows_by_four(w2[e])[:, :, columns])
+
+        nc.sync.dma_start(out=x_first[:], in_=rows_by_four(xT[:K_PASS, :]))
+        nc.sync.dma_start(offsets[:], offs)
+        nc.sync.dma_start(out=gate_rows[0:E, :], in_=gate[0:1, :].rearrange("r (e c) -> (r e) c", e=E))
+        for h in range(2):
+            nc.sync.dma_start(out=x_halves[h][:], in_=rows_by_four(xT[K_PASS:, :])[:, :, h * HALF_T : (h + 1) * HALF_T])
         for e in range(E):
             for s in range(PASSES):
-                nc.sync.dma_start(out=w1_raw[e][:, s], in_=rows_by_four(w1[e][s * K_PASS : (s + 1) * K_PASS, :]))
-            if e < E - 2:
-                nc.sync.dma_start(out=w2_raw[e], in_=rows_by_four(w2[e]))
-            if e == E - 2:
-                nc.sync.dma_start(out=w2_raw[e], in_=rows_by_four(w2[e])[:, :, :HALF_N])
-        nc.sync.dma_start(out=w2_late[E - 2], in_=rows_by_four(w2[E - 2])[:, :, HALF_N:])
-        nc.sync.dma_start(out=w2_raw[E - 1], in_=rows_by_four(w2[E - 1])[:, :, :HALF_N])
-        nc.sync.dma_start(out=w2_late[E - 1], in_=rows_by_four(w2[E - 1])[:, :, HALF_N:])
-        two_tiles = xr[: 2 * P, :].rearrange("(n p) t -> p n t", p=P)
-        nc.sync.dma_start(out=second_halves[:], in_=two_tiles[:, :, HALF_T:])
-        nc.sync.dma_start(out=first_halves[:], in_=two_tiles[:, :, :HALF_T])
-        for n in (2, 3):
-            nc.sync.dma_start(out=residual[n], in_=xr[n * P : (n + 1) * P, :])
+                nc.sync.dma_start(out=w1_raw[e][s][:], in_=rows_by_four(w1[e][s * K_PASS : (s + 1) * K_PASS, :]))
+            load_w2(e, 0)
+        load_w2(last, 1)
+        load_w2(last - 1, 1)
+        for h in range(2):
+            nc.sync.dma_start(out=residual[h][:], in_=xr[h * 2 * P : (h + 1) * 2 * P, :].rearrange("(n p) t -> p n t", p=P))
 
         turned_gate = psum.tile([P, P], F32, name="bank6")
         nc.tensor.transpose(turned_gate[:], gate_rows[:], identity[:])
@@ -111,239 +108,161 @@ def tile_moe_res_mlp_relu_kernel(tc, xT, xr, w1, w2, gate, offs, out):
         def slot_offsets(first_slot, end_slot):
             return offsets[:, first_slot // 16 : end_slot // 16]
 
+        def fresh(shape, dtype, name):
+            return ring.tile(shape, dtype, name=name, align_bytes=64)
+
         for s in range(PASSES):
             for half in range(2):
                 tokens = slice(half * HALF_T, (half + 1) * HALF_T)
-                grouped = ring.tile([P, HALF_T * J], BF16, name="x_grouped", align_bytes=64)
+                grouped = fresh([P, HALF_T * J], BF16, "x_grouped")
                 target = grouped[:].rearrange("p (c i j) -> p c j i", i=4, j=J)
-                source = x_raw[s][:, :, tokens].rearrange("p j (c i) -> p c j i", i=4)
+                source = x_raw[s][half].rearrange("p j (c i) -> p c j i", i=4)
                 nc.scalar.copy(out=target[:, :X_SCALAR_RUNS], in_=source[:, :X_SCALAR_RUNS])
                 nc.vector.tensor_copy(out=target[:, X_SCALAR_RUNS:], in_=source[:, X_SCALAR_RUNS:])
                 quantise(grouped[:], x_codes[s][:, tokens], x_scales[4 * s : P, tokens])
-            if s == 0:
-                codes_pass0 = keep.tile([P, S], U32, name="codes_pass0", align_bytes=64)
-                nc.vector.tensor_copy(codes_pass0[:], x_codes[0][:].indirect(offsets[:]))
-        codes_pass1 = keep.tile([P, S], U32, name="codes_first", align_bytes=64)
-        scales_first = keep.tile([P, C], U8, name="scales_first", align_bytes=64)
-        nc.vector.tensor_copy(codes_pass1[:], x_codes[1][:].indirect(slot_offsets(0, S)))
-        nc.vector.tensor_copy(scales_first[:], x_scales[:].indirect(slot_offsets(0, C)))
-        scales_rest = first.tile([P, S - C], U8, name="scales_rest", align_bytes=64, offset=0)
+            nc.vector.tensor_copy(slot_codes[s][:], x_codes[s][:].indirect(offsets[:]))
+        nc.vector.tensor_copy(slot_scales[:], x_scales[:].indirect(offsets[:]))
 
-        def slot_operand(e, s):
-            codes = (codes_pass0, codes_pass1)[s][:, e * C : (e + 1) * C]
-            scales = scales_first[4 * s : P, :] if e == 0 else scales_rest[4 * s : P, (e - 1) * C : e * C]
-            return codes, scales
-
-        def quantise_w1(e):
-            grouped = ring.tile([P, PASSES, H * J], BF16, name="w1_grouped", align_bytes=64)
-            target = grouped[:].rearrange("p s (t m j) -> p s m j t", t=4, j=J)
-            source = w1_raw[e][:].rearrange("p s j (m t) -> p s m j t", t=4)
-
-            def rounded(copy, passes, first_run, end_run):
-                copy(out=target[:, passes, first_run:end_run], in_=source[:, passes, first_run:end_run])
-
-            cuts = (RUNS - (FIRST_VECTOR_RUNS if e == 0 else PASS0_VECTOR_RUNS), RUNS - PASS1_VECTOR_RUNS)
-            rounded(nc.scalar.copy, 0, JOINT_RUNS, JOINT_RUNS + SLOT_RUNS)
-            rounded(nc.scalar.copy, 0, JOINT_RUNS + SLOT_RUNS, cuts[0])
-            rounded(nc.vector.tensor_copy, 0, cuts[0], RUNS)
-            rounded(nc.scalar.copy, slice(0, PASSES), 0, JOINT_RUNS)
-            rounded(nc.scalar.copy, 1, JOINT_RUNS, SLOT_RUNS)
-            rounded(nc.scalar.copy, 1, SLOT_RUNS, cuts[1])
-            rounded(nc.vector.tensor_copy, 1, cuts[1], RUNS)
-            codes = ring.tile([P, PASSES, H], U32, name="w1_codes", align_bytes=64)
-            scales = ring.tile([P, PASSES, H], U8, name="w1_scales", align_bytes=64)
-            quantise(grouped[:, 0], codes[:, 0], scales[:, 0])
-            for half in range(2):
-                columns = slice(half * H // 2, (half + 1) * H // 2)
-                values = slice(half * H * J // 2, (half + 1) * H * J // 2)
-                quantise(grouped[:, 1, values], codes[:, 1, columns], scales[:, 1, columns])
-            return codes, scales
+        def round_w1(copy, e, s, grouped, first_run, end_run):
+            target = grouped[:].rearrange("p (t m j) -> p m j t", t=4, j=J)
+            source = w1_raw[e][s][:].rearrange("p j (m t) -> p m j t", t=4)
+            copy(out=target[:, first_run:end_run], in_=source[:, first_run:end_run])
 
         def first_layer(e, codes, scales):
             acc = psum.tile([P, J, C], F32, name=f"bank{e % 2}")
+            slots = slice(e * C, (e + 1) * C)
             for s in range(PASSES):
                 for t in range(J):
                     channels = slice(t * P, (t + 1) * P)
-                    x_words, x_bytes = slot_operand(e, s)
                     nc.tensor.matmul_mx(
                         out=acc[:, t, :],
-                        lhsT=codes[:, s, channels].bitcast(FP8X4),
-                        lhsT_scale=scales[:, s, channels],
-                        rhs=x_words.bitcast(FP8X4),
-                        rhs_scale=x_bytes,
+                        lhsT=codes[s][:, channels].bitcast(FP8X4),
+                        lhsT_scale=scales[s][:, channels],
+                        rhs=slot_codes[s][:, slots].bitcast(FP8X4),
+                        rhs_scale=slot_scales[4 * s : P, slots],
                         start=(s == 0 and t == 0),
                         stop=(s == PASSES - 1 and t == J - 1),
                     )
             return acc
 
-        def quantise_hidden(acc, hidden):
+        def rectify(acc):
+            hidden = keep.tile([P, C * J], BF16, name="hidden", align_bytes=64)
             nc.scalar.activation(
-                out=hidden.rearrange("p (c t) -> p c t", t=J),
-                in_=acc[:].rearrange("p t c -> p c t"),
-                func=RELU,
+                out=hidden[:].rearrange("p (c t) -> p c t", t=J), in_=acc[:].rearrange("p t c -> p c t"), func=RELU
             )
-            h_codes = ring.tile([P, C], U32, name="h_codes", align_bytes=64)
-            h_scales = ring.tile([P, C], U8, name="h_scales", align_bytes=64)
-            quantise(hidden, h_codes[:], h_scales[:])
-            return h_codes, h_scales
+            return hidden
 
-        def round_w2(e, grouped, first_column, end_column):
-            if e in w2_late and first_column >= HALF_N:
-                source = w2_late[e][:, :, first_column - HALF_N : end_column - HALF_N]
-            else:
-                source = w2_raw[e][:, :, first_column:end_column]
-            nc.scalar.copy(
-                out=grouped.rearrange("p (c i j) -> p c j i", i=4, j=J),
-                in_=source.rearrange("p j (c i) -> p c j i", i=4),
+        def quantise_hidden(e, hidden):
+            h_codes = keep.tile([P, C], U32, name=f"h_codes{e}", align_bytes=64)
+            h_scales = keep.tile([P, C], U8, name=f"h_scales{e}", align_bytes=64)
+            quantise(hidden[:], h_codes[:], h_scales[:])
+            hidden_mx.append((h_codes, h_scales))
+
+        def round_w2(copy, e, first_tile, end_tile, name, pool=ring):
+            piece = max(i for i, cut in enumerate(w2_cuts[e][:-1]) if cut <= first_tile * P)
+            first = first_tile * P - w2_cuts[e][piece]
+            width = (end_tile - first_tile) * P
+            grouped = pool.tile([P, width * J], BF16, name=name, align_bytes=64)
+            copy(
+                out=grouped[:].rearrange("p (c i j) -> p c j i", i=4, j=J),
+                in_=w2_raw[e][piece][:, :, first : first + width].rearrange("p j (c i) -> p c j i", i=4),
             )
+            return grouped
 
-        def second_layer(bank, tiles, codes, scales, h_codes, h_scales):
-            acc = psum.tile([P, len(tiles), C], F32, name=f"bank{bank}")
-            for i, n in enumerate(tiles):
+        def quantise_w2(e, first_tile, end_tile, grouped):
+            columns = slice(first_tile * P, end_tile * P)
+            quantise(grouped[:], w2_codes[e][:, columns], w2_scales[e][:, columns])
+
+        def second_layer(bank, jobs):
+            acc = psum.tile([P, len(jobs), C], F32, name=f"bank{bank}")
+            for i, (e, n) in enumerate(jobs):
                 nc.tensor.matmul_mx(
                     out=acc[:, i, :],
-                    lhsT=codes[:, n * P : (n + 1) * P].bitcast(FP8X4),
-                    lhsT_scale=scales[:, n * P : (n + 1) * P],
-                    rhs=h_codes[:].bitcast(FP8X4),
-                    rhs_scale=h_scales[:],
+                    lhsT=w2_codes[e][:, n * P : (n + 1) * P].bitcast(FP8X4),
+                    lhsT_scale=w2_scales[e][:, n * P : (n + 1) * P],
+                    rhs=hidden_mx[e][0][:].bitcast(FP8X4),
+                    rhs_scale=hidden_mx[e][1][:],
                     start=True,
                     stop=True,
                 )
             return acc
 
-        def scatter(e, tiles, acc, y):
-            nc.scalar.copy(out=y, in_=acc[:])
+        def gated(e, acc, tiles, y):
+            nc.vector.tensor_tensor(y, acc[:], gates[:, e : e + 1, :].to_broadcast([P, tiles, C]), MULT)
+
+        def scatter(n, first_slot, end_slot, y):
+            nc.scalar.activation(out=windows[n][:].indirect(slot_offsets(first_slot, end_slot)), in_=y, func=COPY)
+
+        def scatter_tiles(e, tiles, y):
             for i, n in enumerate(tiles):
-                window = windows[n][:].indirect(slot_offsets(e * C, (e + 1) * C))
-                nc.vector.tensor_tensor(window, y[:, i, :], gates[:, e, :], MULT)
-
-        def finish(engine, n, first_token, end_token, total):
-            tokens = slice(first_token, end_token)
-            addend = first_halves[:, n] if n < 2 else residual[n][:, tokens]
-            engine.tensor_tensor(total, windows[n][:, tokens], addend, ADD)
-            nc.sync.dma_start(out=out[n * P : (n + 1) * P, tokens], in_=total)
-
-        def turn(source, banks, opens):
-            for block in range(4):
-                nc.tensor.matmul(
-                    banks[block // 2][:, block % 2, :],
-                    source[:, block * P : (block + 1) * P],
-                    identity[:],
-                    is_transpose=True,
-                    start=(opens and block % 2 == 0),
-                    stop=(not opens and block % 2 == 1),
-                )
-
-        def finish_on_tensor(n):
-            banks = [psum.tile([P, 2, P], F32, name=f"bank{4 + 2 * n + pair}") for pair in range(2)]
-            turn(second_halves[:, n], banks, True)
-            turn(windows[n][:, HALF_T:], banks, False)
-            turned = [ring.tile([P, 2, P], F32, name=f"turned{pair}") for pair in range(2)]
-            for pair in range(2):
-                nc.scalar.copy(out=turned[pair][:], in_=banks[pair][:])
-            back = psum.tile([P, J, P], F32, name=f"bank{1 + n}")
-            for b in range(J):
-                nc.tensor.transpose(back[:, b, :], turned[b // 2][:, b % 2, :], identity[:])
-            result = ring.tile([P, HALF_T], F32, name="result")
-            nc.scalar.copy(out=result[:], in_=back[:].rearrange("p b c -> p (b c)"))
-            nc.scalar.dma_start(out=out[n * P : (n + 1) * P, HALF_T:], in_=result[:])
-
-        def w2_tiles():
-            codes = ring.tile([P, N], U32, name="w2_codes", align_bytes=64)
-            scales = ring.tile([P, N], U8, name="w2_scales", align_bytes=64)
-            return codes, scales
-
-        def quantise_columns(e, grouped, first_column, end_column):
-            quantise(grouped, w2_mx[e][0][:, first_column:end_column], w2_mx[e][1][:, first_column:end_column])
-
-        def quantise_w2(e, grouped, first_column, end_column):
-            round_w2(e, grouped, first_column, end_column)
-            quantise_columns(e, grouped, first_column, end_column)
-
-        def fresh(shape, dtype, name):
-            return ring.tile(shape, dtype, name=name, align_bytes=64)[:]
-
-        def products(bank, e, tiles):
-            return second_layer(bank, tiles, *w2_mx[e], *hidden_mx[e])
+                scatter(n, e * C, (e + 1) * C, y[:, i, :])
 
         hidden_mx = []
-        w2_mx = []
-        last = E - 1
-        for e in range(last):
-            w1_codes, w1_scales = quantise_w1(e)
+        waiting = []
+        for e in range(E):
+            grouped = [fresh([P, H * J], BF16, f"w1_grouped{s}") for s in range(PASSES)]
+            codes = [fresh([P, H], U32, f"w1_codes{s}") for s in range(PASSES)]
+            scales = [fresh([P, H], U8, f"w1_scales{s}") for s in range(PASSES)]
             if e == 0:
-                nc.vector.tensor_copy(scales_rest[:], x_scales[:].indirect(slot_offsets(C, S)))
+                round_w1(nc.scalar.copy, e, 0, grouped[0], 0, RUNS)
             else:
-                quantise_w2(e - 1, w1_raw[e][:, 0, 1, 0 : 2 * P].bitcast(BF16), N - P, N)
-                scatter(e - 1, (1, 2), middle_sums, w1_raw[e][:, 1, 0:2, 0:C])
-            acc = first_layer(e, w1_codes, w1_scales)
-            if e > 0:
-                last_sums = products(7, e - 1, (3,))
-            grouped = fresh([P, N * J], BF16, "w2_grouped")
-            w2_mx.append(w2_tiles())
-            quantise_w2(e, grouped[:, : HALF_N * J], 0, HALF_N)
-            if e < last - 1:
-                round_w2(e, grouped[:, HALF_N * J : W2_BEFORE_RELU * J], HALF_N, W2_BEFORE_RELU)
-                hidden_mx.append(quantise_hidden(acc, w2_raw[e][:, 0, 0:HALF_N].bitcast(BF16)))
+                round_w1(nc.scalar.copy, e, 0, grouped[0], 0, SLOT_RUNS)
+                round_w1(nc.vector.tensor_copy, e, 0, grouped[0], PASS0_SCALAR_RUNS, RUNS)
+                round_w1(nc.scalar.copy, e, 0, grouped[0], SLOT_RUNS, PASS0_SCALAR_RUNS)
+                sums, tiles = waiting[0]
+                y = w1_raw[e][0][:, 0 : len(tiles), 0:C]
+                gated(e - 1, sums, len(tiles), y)
+                scatter_tiles(e - 1, tiles, y)
+            quantise(grouped[0][:], codes[0][:], scales[0][:])
+            if e == 0:
+                round_w1(nc.scalar.copy, e, 1, grouped[1], 0, FIRST_SCALAR_RUNS)
+                round_w1(nc.vector.tensor_copy, e, 1, grouped[1], FIRST_SCALAR_RUNS, RUNS)
             else:
-                hidden_mx.append(quantise_hidden(acc, fresh([P, C * J], BF16, "hidden")))
-            if e > 0:
-                scatter(e - 1, (3,), last_sums, w2_raw[e][:, 1:2, 0:C])
-            if e < last - 1:
-                round_w2(e, grouped[:, W2_BEFORE_RELU * J : (N - P) * J], W2_BEFORE_RELU, N - P)
-                quantise_columns(e, grouped[:, HALF_N * J : (N - P) * J], HALF_N, N - P)
-                first_sums = products(2, e, (0,))
-                middle_sums = products(3, e, (1, 2))
-                scatter(e, (0,), first_sums, fresh([P, 1, C], F32, "y_first"))
-            else:
-                first_sums = products(2, e, (0,))
-                middle_sums = products(3, e, (1,))
+                round_w1(nc.vector.tensor_copy, e, 1, grouped[1], 0, RUNS)
+                sums, tiles = waiting[1]
+                y = w1_raw[e][1][:, 0:1, 0:C]
+                gated(e - 1, sums, 1, y)
+                scatter_tiles(e - 1, tiles, y)
+            for half in range(2):
+                columns = slice(half * H // 2, (half + 1) * H // 2)
+                values = slice(half * H * J // 2, (half + 1) * H * J // 2)
+                quantise(grouped[1][:, values], codes[1][:, columns], scales[1][:, columns])
+            acc = first_layer(e, codes, scales)
+            hidden = rectify(acc)
+            loaded = w2_cuts[e][1] // P
+            front = round_w2(nc.vector.tensor_copy, e, 0, 2, "w2_front")
+            if e < last:
+                back = round_w2(nc.vector.tensor_copy, e, 2, loaded, "w2_back")
+            quantise_w2(e, 0, 2, front)
+            quantise_hidden(e, hidden)
+            if e < last:
+                quantise_w2(e, 2, loaded, back)
+                tiles = range(loaded - 1)
+                waiting = [
+                    (second_layer(2, [(e, n) for n in tiles]), tiles),
+                    (second_layer(3, [(e, loaded - 1)]), (loaded - 1,)),
+                ]
 
-        w1_codes, w1_scales = quantise_w1(last)
-        scatter(last - 1, (0,), first_sums, w1_raw[last][:, 1, 0:1, 0:C])
-        quantise_w2(last - 1, grouped[:, HALF_N * J : (N - P) * J], HALF_N, N - P)
-        scatter(last - 1, (1,), middle_sums, w2_late[last - 1][:, 0:1, 0:C])
-        acc = first_layer(last, w1_codes, w1_scales)
-        third_sums = products(2, last - 1, (2,))
-        grouped = fresh([P, N * J], BF16, "w2_grouped")
-        w2_mx.append(w2_tiles())
-        round_w2(last, grouped[:, : P * J], 0, P)
-        round_w2(last, grouped[:, P * J : HALF_N * J], P, HALF_N)
-        quantise_columns(last, grouped[:, : HALF_N * J], 0, HALF_N)
-        hidden_mx.append(quantise_hidden(acc, w2_last[:, : 2 * P].bitcast(BF16)))
-        scatter(last - 1, (2,), third_sums, w2_raw[last][:, 1:2, 0:C])
-        scatter(last, (0,), products(3, last, (0,)), fresh([P, 1, C], F32, "y_last0"))
-        second_sums = products(2, last, (1,))
-        for n in (2, 3):
-            quantise_w2(last, grouped[:, n * P * J : (n + 1) * P * J], n * P, (n + 1) * P)
-        held_grouped = w2_raw[last][:, 2, 0:HALF_N].bitcast(BF16)
-        round_w2(last - 1, held_grouped, N - P, N)
-        gated = w2_late[last - 1][:, 0:2, C:]
-        nc.vector.tensor_tensor(gated[:, 0, :], second_sums[:, 0, :], gates[:, last, :], MULT)
-        nc.vector.tensor_tensor(gated[:, 1, :], products(3, last, (2,))[:, 0, :], gates[:, last, :], MULT)
-        quantise_columns(last - 1, held_grouped, N - P, N)
-        for i in range(2):
-            nc.vector.tensor_copy(windows[1 + i][:].indirect(slot_offsets(last * C, S)), gated[:, i, :])
-        pair_sums = psum.tile([P, 2, C], F32, name="bank0")
-        for e in (last, last - 1):
-            nc.tensor.matmul_mx(
-                out=pair_sums[:, e - last + 1, :],
-                lhsT=w2_mx[e][0][:, N - P :].bitcast(FP8X4),
-                lhsT_scale=w2_mx[e][1][:, N - P :],
-                rhs=hidden_mx[e][0][:].bitcast(FP8X4),
-                rhs_scale=hidden_mx[e][1][:],
-                start=True,
-                stop=True,
-            )
-        pair = fresh([P, 2, C], F32, "pair")
-        nc.vector.tensor_tensor(pair, pair_sums[:], gates[:, last - 1 :, :], MULT)
-        finish(nc.gpsimd, 0, 0, HALF_T, w2_last[:, P + 2 * HALF_N :])
-        finish_on_tensor(0)
-        nc.vector.tensor_copy(windows[3][:].indirect(slot_offsets((last - 1) * C, S)), pair.rearrange("p e c -> p (e c)"))
-        finish(nc.gpsimd, 1, 0, HALF_T, fresh([P, HALF_T], F32, "second_sum"))
-        finish_on_tensor(1)
-        finish(nc.gpsimd, 2, 0, HALF_T, fresh([P, HALF_T], F32, "third_sum"))
-        finish(nc.vector, 2, HALF_T, T, windows[2][:, :HALF_T])
-        finish(nc.vector, 3, 0, HALF_T, residual[2][:, :HALF_T])
-        finish(nc.vector, 3, HALF_T, 3 * T // 4, residual[2][:, HALF_T : 3 * T // 4])
-        finish(nc.vector, 3, 3 * T // 4, T, residual[2][:, 3 * T // 4 :])
+        back = round_w2(nc.scalar.copy, last, 2, NT, "hidden", keep)
+        held = round_w2(nc.vector.tensor_copy, last - 1, NT - 1, NT, "w2_held")
+        for n in range(2):
+            y = fresh([P, 1, C], F32, "y_single")
+            gated(last, second_layer(4 + n, [(last, n)]), 1, y[:])
+            scatter_tiles(last, (n,), y[:])
+        quantise_w2(last - 1, NT - 1, NT, held)
+        quantise_w2(last, 2, NT, back)
+        y = fresh([P, 1, C], F32, "y_third")
+        gated(last, second_layer(7, [(last, 2)]), 1, y[:])
+        scatter_tiles(last, (2,), y[:])
+        pair_sums = second_layer(6, [(last - 1, 3), (last, 3)])
+        y = fresh([P, 2, C], F32, "y_last")
+        nc.vector.tensor_tensor(y[:], pair_sums[:], gates[:, last - 1 :, :], MULT)
+        scatter(3, (last - 1) * C, S, y[:].rearrange("p e c -> p (e c)"))
+
+        for n in range(NT):
+            cuts = (0, HALF_T, T) if n < NT - 1 else (0, HALF_T, 3 * T // 4, T)
+            for first_token, end_token in zip(cuts, cuts[1:]):
+                tokens = slice(first_token, end_token)
+                total = residual[n // 2][:, n % 2, tokens]
+                nc.vector.tensor_tensor(total, windows[n][:, tokens], total, ADD)
+                nc.sync.dma_start(out=out[n * P : (n + 1) * P, tokens], in_=total)

@@ -53,13 +53,13 @@ def tile_moe_res_mlp_relu_kernel(tc, xT, xr, w1, w2, gate, offs, out):
         slot_scales = keep.tile([P, S], U8, name="slot_scales", align_bytes=64)
         windows = [keep.tile([P, T], F32, name=f"window{n}") for n in range(NT)]
         x_first = big.tile([P, J, T], F32, name="x_first", offset=0)
-        x_halves = [big.tile([P, J, HALF_T], F32, name=f"x_half{h}", offset=(2 + h) * J * HALF_T * 4) for h in range(2)]
-        x_raw = [[x_first[:, :, :HALF_T], x_first[:, :, HALF_T:]], [x_halves[0][:], x_halves[1][:]]]
+        x_second = big.tile([P, J, T], F32, name="x_second", offset=J * T * 4)
+        x_raw = [[x[:, :, :HALF_T], x[:, :, HALF_T:]] for x in (x_first, x_second)]
         residual = [big.tile([P, 2, T], F32, name=f"residual{h}", offset=h * 2 * T * 4) for h in range(2)]
         w1_raw = [
             [keep.tile([P, J, H], F32, name=f"w1_raw{e}_{s}", align_bytes=64) for s in range(PASSES)] for e in range(E)
         ]
-        w2_cuts = [(0, N)] * (E - 2) + [(0, N - P, N), (0, HALF_N, N)]
+        w2_cuts = [(0, N)] * E
         w2_raw = [
             [keep.tile([P, J, b - a], F32, name=f"w2_raw{e}_{a}", align_bytes=64) for a, b in zip(cuts, cuts[1:])]
             for e, cuts in enumerate(w2_cuts)
@@ -83,14 +83,11 @@ def tile_moe_res_mlp_relu_kernel(tc, xT, xr, w1, w2, gate, offs, out):
         nc.sync.dma_start(out=x_first[:], in_=rows_by_four(xT[:K_PASS, :]))
         nc.sync.dma_start(offsets[:], offs)
         nc.sync.dma_start(out=gate_rows[0:E, :], in_=gate[0:1, :].rearrange("r (e c) -> (r e) c", e=E))
-        for h in range(2):
-            nc.sync.dma_start(out=x_halves[h][:], in_=rows_by_four(xT[K_PASS:, :])[:, :, h * HALF_T : (h + 1) * HALF_T])
+        nc.sync.dma_start(out=x_second[:], in_=rows_by_four(xT[K_PASS:, :]))
         for e in range(E):
             for s in range(PASSES):
                 nc.sync.dma_start(out=w1_raw[e][s][:], in_=rows_by_four(w1[e][s * K_PASS : (s + 1) * K_PASS, :]))
             load_w2(e, 0)
-        load_w2(last, 1)
-        load_w2(last - 1, 1)
         for h in range(2):
             nc.sync.dma_start(out=residual[h][:], in_=xr[h * 2 * P : (h + 1) * 2 * P, :].rearrange("(n p) t -> p n t", p=P))
 
@@ -229,14 +226,14 @@ def tile_moe_res_mlp_relu_kernel(tc, xT, xr, w1, w2, gate, offs, out):
                 quantise(grouped[1][:, values], codes[1][:, columns], scales[1][:, columns])
             acc = first_layer(e, codes, scales)
             hidden = rectify(acc)
-            loaded = w2_cuts[e][1] // P
+            loaded = NT if e < last - 1 else NT - 1
             front = round_w2(nc.vector.tensor_copy, e, 0, 2, "w2_front")
             if e < last:
-                back = round_w2(nc.vector.tensor_copy, e, 2, loaded, "w2_back")
+                back = round_w2(nc.vector.tensor_copy, e, 2, NT, "w2_back")
             quantise_w2(e, 0, 2, front)
             quantise_hidden(e, hidden)
             if e < last:
-                quantise_w2(e, 2, loaded, back)
+                quantise_w2(e, 2, NT, back)
                 tiles = range(loaded - 1)
                 waiting = [
                     (second_layer(2, [(e, n) for n in tiles]), tiles),
@@ -244,12 +241,10 @@ def tile_moe_res_mlp_relu_kernel(tc, xT, xr, w1, w2, gate, offs, out):
                 ]
 
         back = round_w2(nc.scalar.copy, last, 2, NT, "hidden", keep)
-        held = round_w2(nc.vector.tensor_copy, last - 1, NT - 1, NT, "w2_held")
         for n in range(2):
             y = fresh([P, 1, C], F32, "y_single")
             gated(last, second_layer(4 + n, [(last, n)]), 1, y[:])
             scatter_tiles(last, (n,), y[:])
-        quantise_w2(last - 1, NT - 1, NT, held)
         quantise_w2(last, 2, NT, back)
         y = fresh([P, 1, C], F32, "y_third")
         gated(last, second_layer(7, [(last, 2)]), 1, y[:])
@@ -263,6 +258,7 @@ def tile_moe_res_mlp_relu_kernel(tc, xT, xr, w1, w2, gate, offs, out):
             cuts = (0, HALF_T, T) if n < NT - 1 else (0, HALF_T, 3 * T // 4, T)
             for first_token, end_token in zip(cuts, cuts[1:]):
                 tokens = slice(first_token, end_token)
-                total = residual[n // 2][:, n % 2, tokens]
-                nc.vector.tensor_tensor(total, windows[n][:, tokens], total, ADD)
+                addend = residual[n // 2][:, n % 2, tokens]
+                total = gates[:].rearrange("p e c -> p (e c)") if (n, first_token) == (0, HALF_T) else addend
+                nc.vector.tensor_tensor(total, windows[n][:, tokens], addend, ADD)
                 nc.sync.dma_start(out=out[n * P : (n + 1) * P, tokens], in_=total)

@@ -30,7 +30,7 @@ SLOT_RUNS = C // 4
 
 X_SCALAR_RUNS = 48
 FIRST_SCALAR_RUNS = 64
-PASS0_SCALAR_RUNS = 72
+PASS0_SCALAR_RUNS = 56
 
 
 def tile_moe_res_mlp_relu_kernel(tc, xT, xr, w1, w2, gate, offs, out):
@@ -120,10 +120,10 @@ def tile_moe_res_mlp_relu_kernel(tc, xT, xr, w1, w2, gate, offs, out):
             nc.vector.tensor_copy(slot_codes[s][:], x_codes[s][:].indirect(offsets[:]))
         nc.vector.tensor_copy(slot_scales[:], x_scales[:].indirect(offsets[:]))
 
-        def round_w1(copy, e, s, grouped, first_run, end_run):
+        def round_w1(copy, e, s, grouped, first_run, end_run, results=slice(0, J)):
             target = grouped[:].rearrange("p (t m j) -> p m j t", t=4, j=J)
             source = w1_raw[e][s][:].rearrange("p j (m t) -> p m j t", t=4)
-            copy(out=target[:, first_run:end_run], in_=source[:, first_run:end_run])
+            copy(out=target[:, first_run:end_run, :, results], in_=source[:, first_run:end_run, :, results])
 
         def first_layer(e, codes, scales):
             acc = psum.tile([P, J, C], F32, name=f"bank{e % 2}")
@@ -142,8 +142,7 @@ def tile_moe_res_mlp_relu_kernel(tc, xT, xr, w1, w2, gate, offs, out):
                     )
             return acc
 
-        def rectify(acc):
-            hidden = keep.tile([P, C * J], BF16, name="hidden", align_bytes=64)
+        def rectify(acc, hidden):
             nc.scalar.activation(
                 out=hidden[:].rearrange("p (c t) -> p c t", t=J), in_=acc[:].rearrange("p t c -> p c t"), func=RELU
             )
@@ -155,11 +154,10 @@ def tile_moe_res_mlp_relu_kernel(tc, xT, xr, w1, w2, gate, offs, out):
             quantise(hidden[:], h_codes[:], h_scales[:])
             hidden_mx.append((h_codes, h_scales))
 
-        def round_w2(copy, e, first_tile, end_tile, name, pool=ring):
+        def round_w2(copy, e, first_tile, end_tile, grouped):
             piece = max(i for i, cut in enumerate(w2_cuts[e][:-1]) if cut <= first_tile * P)
             first = first_tile * P - w2_cuts[e][piece]
             width = (end_tile - first_tile) * P
-            grouped = pool.tile([P, width * J], BF16, name=name, align_bytes=64)
             copy(
                 out=grouped[:].rearrange("p (c i j) -> p c j i", i=4, j=J),
                 in_=w2_raw[e][piece][:, :, first : first + width].rearrange("p j (c i) -> p c j i", i=4),
@@ -194,6 +192,13 @@ def tile_moe_res_mlp_relu_kernel(tc, xT, xr, w1, w2, gate, offs, out):
             for i, n in enumerate(tiles):
                 scatter(n, e * C, (e + 1) * C, y[:, i, :])
 
+        def release(e, sums, tiles, y):
+            gated(e, sums, len(tiles), y)
+            scatter_tiles(e, tiles, y)
+
+        def products(e, first_bank, groups):
+            return [(second_layer(first_bank + i, [(e, n) for n in tiles]), tiles) for i, tiles in enumerate(groups)]
+
         hidden_mx = []
         waiting = []
         for e in range(E):
@@ -206,59 +211,36 @@ def tile_moe_res_mlp_relu_kernel(tc, xT, xr, w1, w2, gate, offs, out):
                 round_w1(nc.scalar.copy, e, 0, grouped[0], 0, SLOT_RUNS)
                 round_w1(nc.vector.tensor_copy, e, 0, grouped[0], PASS0_SCALAR_RUNS, RUNS)
                 round_w1(nc.scalar.copy, e, 0, grouped[0], SLOT_RUNS, PASS0_SCALAR_RUNS)
-                sums, tiles = waiting[0]
-                y = w1_raw[e][0][:, 0 : len(tiles), 0:C]
-                gated(e - 1, sums, len(tiles), y)
-                scatter_tiles(e - 1, tiles, y)
+                for sums, tiles in waiting:
+                    release(e - 1, sums, tiles, w1_raw[e][0][:, tiles[0] : tiles[-1] + 1, 0:C])
             quantise(grouped[0][:], codes[0][:], scales[0][:])
             if e == 0:
                 round_w1(nc.scalar.copy, e, 1, grouped[1], 0, FIRST_SCALAR_RUNS)
                 round_w1(nc.vector.tensor_copy, e, 1, grouped[1], FIRST_SCALAR_RUNS, RUNS)
             else:
-                round_w1(nc.vector.tensor_copy, e, 1, grouped[1], 0, RUNS)
-                sums, tiles = waiting[1]
-                y = w1_raw[e][1][:, 0:1, 0:C]
-                gated(e - 1, sums, 1, y)
-                scatter_tiles(e - 1, tiles, y)
+                for half in range(2):
+                    round_w1(nc.vector.tensor_copy, e, 1, grouped[1], 0, RUNS, slice(2 * half, 2 * half + 2))
             for half in range(2):
                 columns = slice(half * H // 2, (half + 1) * H // 2)
                 values = slice(half * H * J // 2, (half + 1) * H * J // 2)
                 quantise(grouped[1][:, values], codes[1][:, columns], scales[1][:, columns])
-            acc = first_layer(e, codes, scales)
-            hidden = rectify(acc)
-            loaded = NT if e < last - 1 else NT - 1
-            front = round_w2(nc.vector.tensor_copy, e, 0, 2, "w2_front")
-            if e < last:
-                back = round_w2(nc.vector.tensor_copy, e, 2, NT, "w2_back")
+            hidden = rectify(first_layer(e, codes, scales), fresh([P, C * J], BF16, "hidden"))
+            front = round_w2(nc.vector.tensor_copy, e, 0, 2, fresh([P, HALF_N * J], BF16, "w2_front"))
+            back = round_w2(nc.vector.tensor_copy, e, 2, NT, fresh([P, HALF_N * J], BF16, "w2_back"))
             quantise_w2(e, 0, 2, front)
             quantise_hidden(e, hidden)
-            if e < last:
-                quantise_w2(e, 2, NT, back)
-                tiles = range(loaded - 1)
-                waiting = [
-                    (second_layer(2, [(e, n) for n in tiles]), tiles),
-                    (second_layer(3, [(e, loaded - 1)]), (loaded - 1,)),
-                ]
+            quantise_w2(e, 2, NT, back)
+            waiting = products(e, 2, [(0,), (1, 2, 3)])
 
-        back = round_w2(nc.scalar.copy, last, 2, NT, "hidden", keep)
-        for n in range(2):
-            y = fresh([P, 1, C], F32, "y_single")
-            gated(last, second_layer(4 + n, [(last, n)]), 1, y[:])
-            scatter_tiles(last, (n,), y[:])
-        quantise_w2(last, 2, NT, back)
-        y = fresh([P, 1, C], F32, "y_third")
-        gated(last, second_layer(7, [(last, 2)]), 1, y[:])
-        scatter_tiles(last, (2,), y[:])
-        pair_sums = second_layer(6, [(last - 1, 3), (last, 3)])
-        y = fresh([P, 2, C], F32, "y_last")
-        nc.vector.tensor_tensor(y[:], pair_sums[:], gates[:, last - 1 :, :], MULT)
-        scatter(3, (last - 1) * C, S, y[:].rearrange("p e c -> p (e c)"))
+        y = fresh([P, NT, C], F32, "y_last")
+        for sums, tiles in waiting:
+            release(last, sums, tiles, y[:, tiles[0] : tiles[-1] + 1])
 
         for n in range(NT):
             cuts = (0, HALF_T, T) if n < NT - 1 else (0, HALF_T, 3 * T // 4, T)
             for first_token, end_token in zip(cuts, cuts[1:]):
                 tokens = slice(first_token, end_token)
                 addend = residual[n // 2][:, n % 2, tokens]
-                total = gates[:].rearrange("p e c -> p (e c)") if (n, first_token) == (0, HALF_T) else addend
+                total = addend
                 nc.vector.tensor_tensor(total, windows[n][:, tokens], addend, ADD)
                 nc.sync.dma_start(out=out[n * P : (n + 1) * P, tokens], in_=total)

@@ -31,6 +31,7 @@ SLOT_RUNS = C // 4
 X_SCALAR_RUNS = 48
 FIRST_SCALAR_RUNS = 64
 PASS0_SCALAR_RUNS = 56
+STORE_CUTS = (0, 512, 1024, 1792, 2560, 3328, 4096)
 
 
 def tile_moe_res_mlp_relu_kernel(tc, xT, xr, w1, w2, gate, offs, out):
@@ -55,7 +56,7 @@ def tile_moe_res_mlp_relu_kernel(tc, xT, xr, w1, w2, gate, offs, out):
         x_first = big.tile([P, J, T], F32, name="x_first", offset=0)
         x_second = big.tile([P, J, T], F32, name="x_second", offset=J * T * 4)
         x_raw = [[x[:, :, :HALF_T], x[:, :, HALF_T:]] for x in (x_first, x_second)]
-        residual = [big.tile([P, 2, T], F32, name=f"residual{h}", offset=h * 2 * T * 4) for h in range(2)]
+        residual = big.tile([P, NT * T], F32, name="residual", offset=0)
         w1_raw = [
             [keep.tile([P, J, H], F32, name=f"w1_raw{e}_{s}", align_bytes=64) for s in range(PASSES)] for e in range(E)
         ]
@@ -88,8 +89,10 @@ def tile_moe_res_mlp_relu_kernel(tc, xT, xr, w1, w2, gate, offs, out):
             for s in range(PASSES):
                 nc.sync.dma_start(out=w1_raw[e][s][:], in_=rows_by_four(w1[e][s * K_PASS : (s + 1) * K_PASS, :]))
             load_w2(e, 0)
+        xr_rows = xr.rearrange("(p n) t -> p (n t)", n=NT)
         for h in range(2):
-            nc.sync.dma_start(out=residual[h][:], in_=xr[h * 2 * P : (h + 1) * 2 * P, :].rearrange("(n p) t -> p n t", p=P))
+            columns = slice(h * 2 * T, (h + 1) * 2 * T)
+            nc.sync.dma_start(out=residual[:, columns], in_=xr_rows[:, columns])
 
         turned_gate = psum.tile([P, P], F32, name="bank6")
         nc.tensor.transpose(turned_gate[:], gate_rows[:], identity[:])
@@ -155,12 +158,9 @@ def tile_moe_res_mlp_relu_kernel(tc, xT, xr, w1, w2, gate, offs, out):
             hidden_mx.append((h_codes, h_scales))
 
         def round_w2(copy, e, first_tile, end_tile, grouped):
-            piece = max(i for i, cut in enumerate(w2_cuts[e][:-1]) if cut <= first_tile * P)
-            first = first_tile * P - w2_cuts[e][piece]
-            width = (end_tile - first_tile) * P
             copy(
-                out=grouped[:].rearrange("p (c i j) -> p c j i", i=4, j=J),
-                in_=w2_raw[e][piece][:, :, first : first + width].rearrange("p j (c i) -> p c j i", i=4),
+                out=grouped[:].rearrange("p (t m j) -> p m j t", t=end_tile - first_tile, j=J),
+                in_=w2_raw[e][0][:].rearrange("p j (m t) -> p m j t", t=NT)[:, :, :, first_tile:end_tile],
             )
             return grouped
 
@@ -230,17 +230,16 @@ def tile_moe_res_mlp_relu_kernel(tc, xT, xr, w1, w2, gate, offs, out):
             quantise_w2(e, 0, 2, front)
             quantise_hidden(e, hidden)
             quantise_w2(e, 2, NT, back)
-            waiting = products(e, 2, [(0,), (1, 2, 3)])
+            waiting = products(e, 2, [(0,), (1, 2, 3)] if e < last else [(0,), (1,), (2, 3)])
 
         y = fresh([P, NT, C], F32, "y_last")
         for sums, tiles in waiting:
             release(last, sums, tiles, y[:, tiles[0] : tiles[-1] + 1])
 
-        for n in range(NT):
-            cuts = (0, HALF_T, T) if n < NT - 1 else (0, HALF_T, 3 * T // 4, T)
-            for first_token, end_token in zip(cuts, cuts[1:]):
-                tokens = slice(first_token, end_token)
-                addend = residual[n // 2][:, n % 2, tokens]
-                total = addend
-                nc.vector.tensor_tensor(total, windows[n][:, tokens], addend, ADD)
-                nc.sync.dma_start(out=out[n * P : (n + 1) * P, tokens], in_=total)
+        out_rows = out.rearrange("(p n) t -> p (n t)", n=NT)
+        for first, end in zip(STORE_CUTS, STORE_CUTS[1:]):
+            for n in range(first // T, (end - 1) // T + 1):
+                low, high = max(first, n * T), min(end, (n + 1) * T)
+                total = residual[:, low:high]
+                nc.vector.tensor_tensor(total, windows[n][:, low - n * T : high - n * T], total, ADD)
+            nc.sync.dma_start(out=out_rows[:, first:end], in_=residual[:, first:end])

from contextlib import ExitStack

import concourse.mybir as mybir
from concourse.masks import make_identity

K, T, E, C, H, N = 1024, 1024, 4, 128, 512, 512
S = E * C
FLOPS = 2 * S * (K * H + H * N)

F32 = mybir.dt.float32
BF16 = mybir.dt.bfloat16
U32 = mybir.dt.uint32
U16 = mybir.dt.uint16
U8 = mybir.dt.uint8
FP8X4 = mybir.dt.float8_e4m3fn_x4
ADD = mybir.AluOpType.add
MULT = mybir.AluOpType.mult
RELU = mybir.ActivationFunctionType.Relu
COPY = mybir.ActivationFunctionType.Copy

P = 128
J = 4
K_PASS = P * J
PASSES = K // K_PASS
NT = N // P
HALF_T = T // 2
HALF_N = N // 2
RUNS = H // 4
SLOT_RUNS = C // 4

X_SCALAR_RUNS = 48
FIRST_SCALAR_RUNS = 64
PASS0_SCALAR_RUNS = 56
STORE_CUTS = (0, 512, 1024, 1792, 2560, 3328, 4096)


def tile_moe_res_mlp_relu_kernel(tc, xT, xr, w1, w2, gate, offs, out):
    nc = tc.nc
    last = E - 1
    with ExitStack() as ctx:
        keep = ctx.enter_context(tc.tile_pool(name="keep", bufs=1))
        big = ctx.enter_context(tc.tile_pool(name="big", bufs=1))
        ring = ctx.enter_context(tc.tile_pool(name="ring", bufs=2))
        psum = ctx.enter_context(tc.psum_pool(name="psum", bufs=1))

        offsets = keep.tile([P, S // 16], U16, name="offsets")
        gate_rows = keep.tile([P, C], F32, name="gate_rows")
        gate_columns = keep.tile([P, E], F32, name="gate_columns")
        gates = keep.tile([P, E, C], F32, name="gates")
        identity = keep.tile([P, P], F32, name="identity")
        x_codes = [keep.tile([P, T], U32, name=f"x_codes{s}", align_bytes=64) for s in range(PASSES)]
        x_scales = keep.tile([P, T], U8, name="x_scales", align_bytes=64)
        slot_codes = [keep.tile([P, S], U32, name=f"slot_codes{s}", align_bytes=64) for s in range(PASSES)]
        slot_scales = keep.tile([P, S], U8, name="slot_scales", align_bytes=64)
        windows = [keep.tile([P, T], F32, name=f"window{n}") for n in range(NT)]
        x_first = big.tile([P, J, T], F32, name="x_first", offset=0)
        x_second = big.tile([P, J, T], F32, name="x_second", offset=J * T * 4)
        x_raw = [[x[:, :, :HALF_T], x[:, :, HALF_T:]] for x in (x_first, x_second)]
        residual = big.tile([P, NT * T], F32, name="residual", offset=0)
        w1_raw = [
            [keep.tile([P, J, H], F32, name=f"w1_raw{e}_{s}", align_bytes=64) for s in range(PASSES)] for e in range(E)
        ]
        w2_cuts = [(0, N)] * E
        w2_raw = [
            [keep.tile([P, J, b - a], F32, name=f"w2_raw{e}_{a}", align_bytes=64) for a, b in zip(cuts, cuts[1:])]
            for e, cuts in enumerate(w2_cuts)
        ]
        w2_codes = [keep.tile([P, N], U32, name=f"w2_codes{e}", align_bytes=64) for e in range(E)]
        w2_scales = [keep.tile([P, N], U8, name=f"w2_scales{e}", align_bytes=64) for e in range(E)]

        nc.vector.memset(gate_rows[:], 0.0)
        make_identity(nc, identity[:])
        nc.gpsimd.memset(x_scales[:].bitcast(U32), 0)
        for n in range(NT):
            nc.vector.memset(windows[n][:], 0.0)

        def rows_by_four(matrix):
            return matrix.rearrange("(p j) c -> p j c", j=J)

        def load_w2(e, piece):
            columns = slice(w2_cuts[e][piece], w2_cuts[e][piece + 1])
            nc.sync.dma_start(out=w2_raw[e][piece][:], in_=rows_by_four(w2[e])[:, :, columns])

        nc.sync.dma_start(out=x_first[:], in_=rows_by_four(xT[:K_PASS, :]))
        nc.sync.dma_start(offsets[:], offs)
        nc.sync.dma_start(out=gate_rows[0:E, :], in_=gate[0:1, :].rearrange("r (e c) -> (r e) c", e=E))
        nc.sync.dma_start(out=x_second[:], in_=rows_by_four(xT[K_PASS:, :]))
        for e in range(E):
            for s in range(PASSES):
                nc.sync.dma_start(out=w1_raw[e][s][:], in_=rows_by_four(w1[e][s * K_PASS : (s + 1) * K_PASS, :]))
            load_w2(e, 0)
        xr_rows = xr.rearrange("(p n) t -> p (n t)", n=NT)
        for h in range(2):
            columns = slice(h * 2 * T, (h + 1) * 2 * T)
            nc.sync.dma_start(out=residual[:, columns], in_=xr_rows[:, columns])

        turned_gate = psum.tile([P, P], F32, name="bank6")
        nc.tensor.transpose(turned_gate[:], gate_rows[:], identity[:])
        nc.scalar.copy(out=gate_columns[:], in_=turned_gate[:, 0:E])
        spread_gate = psum.tile([P, E, C], F32, name="bank5")
        for e in range(E):
            nc.tensor.transpose(spread_gate[:, e, :], gate_columns[:, e : e + 1].to_broadcast([P, P]), identity[:])
        nc.scalar.copy(out=gates[:], in_=spread_gate[:])

        def quantise(grouped, codes, scales):
            nc.vector.quantize_mx(out=codes.bitcast(FP8X4), scales=scales, in_=grouped)

        def slot_offsets(first_slot, end_slot):
            return offsets[:, first_slot // 16 : end_slot // 16]

        def fresh(shape, dtype, name):
            return ring.tile(shape, dtype, name=name, align_bytes=64)

        for s in range(PASSES):
            for half in range(2):
                tokens = slice(half * HALF_T, (half + 1) * HALF_T)
                grouped = fresh([P, HALF_T * J], BF16, "x_grouped")
                target = grouped[:].rearrange("p (c i j) -> p c j i", i=4, j=J)
                source = x_raw[s][half].rearrange("p j (c i) -> p c j i", i=4)
                nc.scalar.copy(out=target[:, :X_SCALAR_RUNS], in_=source[:, :X_SCALAR_RUNS])
                nc.vector.tensor_copy(out=target[:, X_SCALAR_RUNS:], in_=source[:, X_SCALAR_RUNS:])
                quantise(grouped[:], x_codes[s][:, tokens], x_scales[4 * s : P, tokens])
            nc.vector.tensor_copy(slot_codes[s][:], x_codes[s][:].indirect(offsets[:]))
        nc.vector.tensor_copy(slot_scales[:], x_scales[:].indirect(offsets[:]))

        def round_w1(copy, e, s, grouped, first_run, end_run, results=slice(0, J)):
            target = grouped[:].rearrange("p (t m j) -> p m j t", t=4, j=J)
            source = w1_raw[e][s][:].rearrange("p j (m t) -> p m j t", t=4)
            copy(out=target[:, first_run:end_run, :, results], in_=source[:, first_run:end_run, :, results])

        def first_layer(e, codes, scales):
            acc = psum.tile([P, J, C], F32, name=f"bank{e % 2}")
            slots = slice(e * C, (e + 1) * C)
            for s in range(PASSES):
                for t in range(J):
                    channels = slice(t * P, (t + 1) * P)
                    nc.tensor.matmul_mx(
                        out=acc[:, t, :],
                        lhsT=codes[s][:, channels].bitcast(FP8X4),
                        lhsT_scale=scales[s][:, channels],
                        rhs=slot_codes[s][:, slots].bitcast(FP8X4),
                        rhs_scale=slot_scales[4 * s : P, slots],
                        start=(s == 0 and t == 0),
                        stop=(s == PASSES - 1 and t == J - 1),
                    )
            return acc

        def rectify(acc, hidden):
            nc.scalar.activation(
                out=hidden[:].rearrange("p (c t) -> p c t", t=J), in_=acc[:].rearrange("p t c -> p c t"), func=RELU
            )
            return hidden

        def quantise_hidden(e, hidden):
            h_codes = keep.tile([P, C], U32, name=f"h_codes{e}", align_bytes=64)
            h_scales = keep.tile([P, C], U8, name=f"h_scales{e}", align_bytes=64)
            quantise(hidden[:], h_codes[:], h_scales[:])
            hidden_mx.append((h_codes, h_scales))

        def round_w2(copy, e, first_tile, end_tile, grouped):
            copy(
                out=grouped[:].rearrange("p (t m j) -> p m j t", t=end_tile - first_tile, j=J),
                in_=w2_raw[e][0][:].rearrange("p j (m t) -> p m j t", t=NT)[:, :, :, first_tile:end_tile],
            )
            return grouped

        def quantise_w2(e, first_tile, end_tile, grouped):
            columns = slice(first_tile * P, end_tile * P)
            quantise(grouped[:], w2_codes[e][:, columns], w2_scales[e][:, columns])

        def second_layer(bank, jobs):
            acc = psum.tile([P, len(jobs), C], F32, name=f"bank{bank}")
            for i, (e, n) in enumerate(jobs):
                nc.tensor.matmul_mx(
                    out=acc[:, i, :],
                    lhsT=w2_codes[e][:, n * P : (n + 1) * P].bitcast(FP8X4),
                    lhsT_scale=w2_scales[e][:, n * P : (n + 1) * P],
                    rhs=hidden_mx[e][0][:].bitcast(FP8X4),
                    rhs_scale=hidden_mx[e][1][:],
                    start=True,
                    stop=True,
                )
            return acc

        def gated(e, acc, tiles, y):
            nc.vector.tensor_tensor(y, acc[:], gates[:, e : e + 1, :].to_broadcast([P, tiles, C]), MULT)

        def scatter(n, first_slot, end_slot, y):
            nc.scalar.activation(out=windows[n][:].indirect(slot_offsets(first_slot, end_slot)), in_=y, func=COPY)

        def scatter_tiles(e, tiles, y):
            for i, n in enumerate(tiles):
                scatter(n, e * C, (e + 1) * C, y[:, i, :])

        def release(e, sums, tiles, y):
            gated(e, sums, len(tiles), y)
            scatter_tiles(e, tiles, y)

        def products(e, first_bank, groups):
            return [(second_layer(first_bank + i, [(e, n) for n in tiles]), tiles) for i, tiles in enumerate(groups)]

        hidden_mx = []
        waiting = []
        for e in range(E):
            grouped = [fresh([P, H * J], BF16, f"w1_grouped{s}") for s in range(PASSES)]
            codes = [fresh([P, H], U32, f"w1_codes{s}") for s in range(PASSES)]
            scales = [fresh([P, H], U8, f"w1_scales{s}") for s in range(PASSES)]
            if e == 0:
                round_w1(nc.scalar.copy, e, 0, grouped[0], 0, RUNS)
            else:
                round_w1(nc.scalar.copy, e, 0, grouped[0], 0, SLOT_RUNS)
                round_w1(nc.vector.tensor_copy, e, 0, grouped[0], PASS0_SCALAR_RUNS, RUNS)
                round_w1(nc.scalar.copy, e, 0, grouped[0], SLOT_RUNS, PASS0_SCALAR_RUNS)
                for sums, tiles in waiting:
                    release(e - 1, sums, tiles, w1_raw[e][0][:, tiles[0] : tiles[-1] + 1, 0:C])
            quantise(grouped[0][:], codes[0][:], scales[0][:])
            if e == 0:
                round_w1(nc.scalar.copy, e, 1, grouped[1], 0, FIRST_SCALAR_RUNS)
                round_w1(nc.vector.tensor_copy, e, 1, grouped[1], FIRST_SCALAR_RUNS, RUNS)
            else:
                for half in range(2):
                    round_w1(nc.vector.tensor_copy, e, 1, grouped[1], 0, RUNS, slice(2 * half, 2 * half + 2))
            for half in range(2):
                columns = slice(half * H // 2, (half + 1) * H // 2)
                values = slice(half * H * J // 2, (half + 1) * H * J // 2)
                quantise(grouped[1][:, values], codes[1][:, columns], scales[1][:, columns])
            hidden = rectify(first_layer(e, codes, scales), fresh([P, C * J], BF16, "hidden"))
            front = round_w2(nc.vector.tensor_copy, e, 0, 2, fresh([P, HALF_N * J], BF16, "w2_front"))
            back = round_w2(nc.vector.tensor_copy, e, 2, NT, fresh([P, HALF_N * J], BF16, "w2_back"))
            quantise_w2(e, 0, 2, front)
            quantise_hidden(e, hidden)
            quantise_w2(e, 2, NT, back)
            waiting = products(e, 2, [(0,), (1, 2, 3)] if e < last else [(0,), (1,), (2, 3)])

        y = fresh([P, NT, C], F32, "y_last")
        for sums, tiles in waiting:
            release(last, sums, tiles, y[:, tiles[0] : tiles[-1] + 1])

        out_rows = out.rearrange("(p n) t -> p (n t)", n=NT)
        for first, end in zip(STORE_CUTS, STORE_CUTS[1:]):
            for n in range(first // T, (end - 1) // T + 1):
                low, high = max(first, n * T), min(end, (n + 1) * T)
                total = residual[:, low:high]
                nc.vector.tensor_tensor(total, windows[n][:, low - n * T : high - n * T], total, ADD)
            nc.sync.dma_start(out=out_rows[:, first:end], in_=residual[:, first:end])
